import numpy as np
import ml_dtypes


def mxq(x, axis, fmt="e4m3"):
    dtype, down = {"e4m3": (ml_dtypes.float8_e4m3fn, 7), "e5m2": (ml_dtypes.float8_e5m2, 14)}[fmt]
    v = np.moveaxis(np.asarray(x, np.float32).astype(ml_dtypes.bfloat16).astype(np.float64), axis, -1)
    blocks = v.reshape(v.shape[:-1] + (-1, 32))
    amax = np.abs(blocks).max(-1, keepdims=True)
    byte = np.maximum(np.where(amax > 0, np.frexp(amax)[1] - 1 + 127, 0) - down, 1)
    scale = np.exp2(byte - 127.0)
    codes = (blocks / scale).astype(np.float32).astype(dtype).astype(np.float64)
    return np.moveaxis((codes * scale).reshape(v.shape), -1, axis)


WIDE = False


def mx_kscale(k):
    if not WIDE:
        return np.ones(k)
    levels = np.array([24, -24, 12, -12, 0])
    if k % 512:
        return np.exp2(np.random.permutation(np.resize(levels, k // 32))).repeat(32)
    a = np.empty((k // 512, 16))
    for p in range(k // 512):
        a[p, :8] = np.random.permutation(np.resize(levels, 8))
        for g in range(8):
            far = levels[np.abs(levels - a[p, g]) >= 10]
            a[p, g + 8] = far[np.random.randint(len(far))]
    return np.exp2(a.ravel()).repeat(32)


def f64(x):
    return np.asarray(x).astype(np.float64)


def striped(idx):
    return np.tile(idx.reshape(-1, 16).T, (8, 1)).astype(np.uint16)


def unstriped(offs):
    return offs[:16].T.reshape(-1).astype(np.int64)


E2M1 = np.array([0.0, 0.5, 1.0, 1.5, 2.0, 3.0, 4.0, 6.0, -0.0, -0.5, -1.0, -1.5, -2.0, -3.0, -4.0, -6.0])


def pack_weight(w, fmt):
    k, n = w.shape
    w = f64(np.asarray(w, np.float32).astype(ml_dtypes.bfloat16)).reshape(k // 32, 32, n)
    amax = np.abs(w).max(1)
    if fmt == "e4m3":
        byte = np.frexp(amax)[1] - 1 + 127 - 7
    else:
        mant, ex = np.frexp(amax / 6.0)
        byte = np.where(mant > 0.5, ex, ex - 1) + 127
    byte = np.clip(np.where(amax > 0, byte, 1), 1, 254)
    scaled = (w * np.exp2(127.0 - byte)[:, None, :]).reshape(k, n).astype(np.float32)
    by_word = np.ascontiguousarray(scaled.reshape(k // 512, 128, 4, n).transpose(0, 1, 3, 2))
    if fmt == "e4m3":
        words = by_word.astype(ml_dtypes.float8_e4m3fn).view(np.uint8)
    else:
        c = by_word.astype(ml_dtypes.float4_e2m1fn).view(np.uint8) & 0xF
        words = (c[..., 0::2] | (c[..., 1::2] << 4)).reshape(k // 512, 128, 2 * n)
    return np.ascontiguousarray(words), np.ascontiguousarray(byte.astype(np.uint8).reshape(k // 512, 16, n))


def unpack_weight(words, scales, fmt):
    g, _, n = scales.shape
    words = np.ascontiguousarray(words).reshape(g, 128, n, -1)
    if fmt == "e4m3":
        vals = words.view(ml_dtypes.float8_e4m3fn).astype(np.float64)
    else:
        nib = np.empty((g, 128, n, 4), np.uint8)
        nib[..., 0::2] = words & 0xF
        nib[..., 1::2] = words >> 4
        vals = E2M1[nib]
    vals = vals * np.repeat(np.exp2(scales.astype(np.float64) - 127.0), 8, axis=1)[..., None]
    return vals.transpose(0, 1, 3, 2).reshape(g * 512, n)


K, N, T, J = 512, 256, 2048, 1024


def setup_inputs():
    n = np.random.standard_normal
    s = mx_kscale(K)[:, None]
    p_tab = pack_weight(n((K, T)) * s, "e4m3")
    p_tab2 = pack_weight(n((K, T)) * s, "e4m3")
    p_wr4 = pack_weight(n((K, N)) / np.sqrt(2 * K) / s, "e2m1")
    return {
        "tab_words": p_tab[0],
        "tab_scales": p_tab[1],
        "tab2_words": p_tab2[0],
        "tab2_scales": p_tab2[1],
        "wr4_words": p_wr4[0],
        "wr4_scales": p_wr4[1],
        "wrd": (0.4 * (n((K, N)) / np.sqrt(2 * K) / s)).astype(np.float32),
        "wi": (n((K, N)) / np.sqrt(2 * K) / s).astype(np.float32),
        "offs": striped(np.random.permutation(T)[:J]),
    }


def reference(tab_words, tab_scales, tab2_words, tab2_scales, wr4_words, wr4_scales, wrd, wi, offs):
    idx = unstriped(offs)
    tab_ = unpack_weight(tab_words, tab_scales, "e4m3")[:, idx]
    tab2_ = unpack_weight(tab2_words, tab2_scales, "e4m3")[:, idx]
    wr4_ = unpack_weight(wr4_words, wr4_scales, "e2m1")
    wrd_ = mxq(f64(wrd), 0, "e4m3")
    wi_ = mxq(f64(wi), 0, "e4m3")
    rr = wr4_.T @ tab_ + wrd_.T @ tab_
    ii = wi_.T @ tab2_
    zr = rr - ii
    ri = wr4_.T @ tab2_ + wrd_.T @ tab2_ + wi_.T @ tab_
    zi = ri
    return (zr) ** 2 + (zi) ** 2

@@ -1,0 +1,161 @@
+from contextlib import ExitStack
+
+import concourse.mybir as mybir
+
+K, N, T, J = 512, 256, 2048, 1024
+FLOPS = 6 * 2 * K * N * J
+
+F32, BF16 = mybir.dt.float32, mybir.dt.bfloat16
+I32, U32, U16, U8 = mybir.dt.int32, mybir.dt.uint32, mybir.dt.uint16, mybir.dt.uint8
+E4M3, E2M1 = mybir.dt.float8_e4m3fn_x4, mybir.dt.float4_e2m1fn_x4
+ACT = mybir.ActivationFunctionType
+ALU = mybir.AluOpType
+
+P = 128
+PACK = 4
+M = 128
+SLICE = 256
+HALF = 128
+STRIPE = 16
+
+
+def tile_list_cpxtab_dl_pow_kernel(
+    tc, tab_words, tab_scales, tab2_words, tab2_scales, wr4_words, wr4_scales, wrd, wi, offs, out
+):
+    nc = tc.nc
+    with ExitStack() as ctx:
+        keep = ctx.enter_context(tc.tile_pool(name="keep", bufs=1))
+        psum = ctx.enter_context(tc.psum_pool(name="psum", bufs=1))
+
+        def sb(shape, dtype, name, **kw):
+            return keep.tile(shape, dtype, name=name, align_bytes=64, **kw)
+
+        def zero_plane(name, width):
+            plane = sb([P, width], U8, name)
+            nc.vector.memset(plane[:].bitcast(I32), 0)
+            return plane
+
+        def load_plane(queue, plane, scales):
+            for q in range(4):
+                queue.dma_start(
+                    out=plane[32 * q : 32 * q + 4, :].bitcast(I32),
+                    in_=scales[0, 4 * q : 4 * q + 4, :].bitcast(I32),
+                )
+
+        def load_words(words, name):
+            tile = sb([P, T], I32, name)
+            nc.sync.dma_start(out=tile[:], in_=words[0].rearrange("p t i -> p (t i)").bitcast(I32))
+            return tile
+
+        def load_weight(w, name):
+            raw = sb([P, PACK, N], F32, name)
+            nc.sync.dma_start(out=raw[:], in_=w.rearrange("(p i) n -> p i n", i=PACK))
+            return raw
+
+        v_plane = sb([P, T], U8, "v_plane")
+        nc.vector.memset(v_plane[:, : T // 2].bitcast(I32), 0)
+        nc.gpsimd.memset(v_plane[:, T // 2 :].bitcast(I32), 0)
+        offsets = keep.tile([P, J // STRIPE], U16, name="offsets")
+        nc.sync.dma_start(offsets[:], offs)
+        wr4_plane = zero_plane("wr4_plane", N)
+        v2_plane = zero_plane("v2_plane", T)
+        wr4_codes = sb([P, 2 * N], U8, "wr4_codes")
+        for m in range(N // M):
+            nc.sync.dma_start(out=wr4_codes[:, 2 * m * M : 2 * (m + 1) * M].bitcast(I32), in_=wr4_words[0, :, 2 * m * M : 2 * (m + 1) * M].bitcast(I32))
+        load_plane(nc.sync, v_plane, tab_scales)
+        v_words = load_words(tab_words, "v_words")
+        load_plane(nc.sync, wr4_plane, wr4_scales)
+        wi_raw = load_weight(wi, "wi_raw")
+        wrd_raw = load_weight(wrd, "wrd_raw")
+        v2_words = load_words(tab2_words, "v2_words")
+        load_plane(nc.sync, v2_plane, tab2_scales)
+
+        def gather(window, dtype, j0, width, name, **kw):
+            picked = sb([P, width], dtype, name, **kw)
+            nc.vector.tensor_copy(
+                picked[:], window.indirect(offsets[:, j0 // STRIPE : (j0 + width) // STRIPE])
+            )
+            return picked
+
+        def interleave(raw, name, sign):
+            grouped = sb([P, N, PACK], BF16, name)
+            dst = grouped[:].rearrange("p (c e) i -> p c i e", e=4)
+            src = raw[:].rearrange("p i (c e) -> p c i e", e=4)
+            nc.scalar.activation(dst, src, ACT.Copy, scale=sign)
+            return grouped
+
+        def quantise(grouped, name):
+            codes = sb([P, N], U32, name + "_codes")
+            plane = sb([P, N], U8, name + "_plane")
+            nc.vector.quantize_mx(
+                out=codes[:].bitcast(E4M3), scales=plane[:], in_=grouped[:].rearrange("p n i -> p (n i)")
+            )
+            return codes, plane
+
+        v_scales = gather(v_plane[:], U8, 0, J, "v_scales")
+        v_picked = [gather(v_words[:].bitcast(U32), U32, j0, J // 2, "v_picked%d" % j0) for j0 in (0, J // 2)]
+        wi_q = quantise(interleave(wi_raw, "wi_bf", 1.0), "wi")
+        wrd_q = quantise(interleave(wrd_raw, "wrd_bf", 1.0), "wrd")
+        nwi_q = quantise(interleave(wi_raw, "nwi_bf", -1.0), "nwi")
+
+        def pass_e4m3(dst, w, m, codes, scales, start=False, stop=False):
+            nc.tensor.matmul_mx(
+                out=dst,
+                lhsT=w[0][:, m * M : (m + 1) * M].bitcast(E4M3),
+                lhsT_scale=w[1][:, m * M : (m + 1) * M],
+                rhs=codes.bitcast(E4M3),
+                rhs_scale=scales,
+                start=start,
+                stop=stop,
+            )
+
+        def passes_e2m1(dst, m, codes, scales, start=False, stop=False):
+            for h in range(SLICE // HALF):
+                cols = slice(h * HALF, (h + 1) * HALF)
+                nc.tensor.matmul_mx(
+                    out=dst[:, cols],
+                    lhsT=wr4_codes[:, 2 * m * M : 2 * (m + 1) * M].bitcast(E2M1),
+                    lhsT_scale=wr4_plane[:, m * M : (m + 1) * M],
+                    rhs=codes[:, cols].bitcast(E4M3),
+                    rhs_scale=scales[:, cols],
+                    start=start and h == 0,
+                    stop=stop and h == SLICE // HALF - 1,
+                )
+
+        slices = J // SLICE
+        banks = {}
+        for s in range(slices):
+            for m in range(N // M):
+                banks[s, m] = psum.tile([P, 2 * SLICE], F32, name="bank%d_%d" % (s, m))
+
+        def v_operand(s):
+            j0 = s * SLICE
+            inner = j0 % (J // 2)
+            return v_picked[j0 // (J // 2)][:, inner : inner + SLICE], v_scales[:, j0 : j0 + SLICE]
+
+        for s in range(slices):
+            for m in range(N // M):
+                passes_e2m1(banks[s, m][:, :SLICE], m, *v_operand(s), start=True)
+        for s in range(slices):
+            for m in range(N // M):
+                pass_e4m3(banks[s, m][:, SLICE:], wi_q, m, *v_operand(s))
+        for s in range(slices):
+            for m in range(N // M):
+                pass_e4m3(banks[s, m][:, :SLICE], wrd_q, m, *v_operand(s))
+
+        for s in range(slices):
+            j0 = s * SLICE
+            scales = gather(v2_plane[:], U8, j0, SLICE, "v2_scales%d" % s, tag="v2_scales", bufs=2)
+            codes = gather(v2_words[:].bitcast(U32), U32, j0, SLICE, "v2_picked%d" % s, tag="v2_picked", bufs=2)
+            for m in range(N // M):
+                bank = banks[s, m]
+                passes_e2m1(bank[:, SLICE:], m, codes[:], scales[:])
+                pass_e4m3(bank[:, SLICE:], wrd_q, m, codes[:], scales[:])
+                pass_e4m3(bank[:, :SLICE], nwi_q, m, codes[:], scales[:], stop=True)
+            for m in range(N // M):
+                squares = sb([P, 2 * SLICE], F32, "squares%d_%d" % (s, m))
+                nc.scalar.activation(squares[:], banks[s, m][:], ACT.Square)
+                power = sb([P, SLICE], F32, "power%d_%d" % (s, m))
+                adder = nc.vector if s == slices - 1 else nc.gpsimd
+                adder.tensor_tensor(power[:], squares[:, :SLICE], squares[:, SLICE:], ALU.add)
+                nc.sync.dma_start(out=out[m * M : (m + 1) * M, j0 : j0 + SLICE], in_=power[:])

@@ -37,7 +37,7 @@ def tile_list_cpxtab_dl_pow_kernel(
 
         def load_plane(queue, plane, scales):
             for q in range(4):
-                queue.dma_start(
+                queue[q].dma_start(
                     out=plane[32 * q : 32 * q + 4, :].bitcast(I32),
                     in_=scales[0, 4 * q : 4 * q + 4, :].bitcast(I32),
                 )
@@ -62,13 +62,13 @@ def tile_list_cpxtab_dl_pow_kernel(
         wr4_codes = sb([P, 2 * N], U8, "wr4_codes")
         for m in range(N // M):
             nc.sync.dma_start(out=wr4_codes[:, 2 * m * M : 2 * (m + 1) * M].bitcast(I32), in_=wr4_words[0, :, 2 * m * M : 2 * (m + 1) * M].bitcast(I32))
-        load_plane(nc.sync, v_plane, tab_scales)
+        load_plane((nc.sync, nc.scalar, nc.sync, nc.scalar), v_plane, tab_scales)
         v_words = load_words(tab_words, "v_words")
-        load_plane(nc.sync, wr4_plane, wr4_scales)
+        load_plane([nc.sync] * 4, wr4_plane, wr4_scales)
         wi_raw = load_weight(wi, "wi_raw")
         wrd_raw = load_weight(wrd, "wrd_raw")
+        load_plane([nc.sync] * 4, v2_plane, tab2_scales)
         v2_words = load_words(tab2_words, "v2_words")
-        load_plane(nc.sync, v2_plane, tab2_scales)
 
         def gather(window, dtype, j0, width, name, **kw):
             picked = sb([P, width], dtype, name, **kw)
@@ -93,7 +93,12 @@ def tile_list_cpxtab_dl_pow_kernel(
             return codes, plane
 
         v_scales = gather(v_plane[:], U8, 0, J, "v_scales")
-        v_picked = [gather(v_words[:].bitcast(U32), U32, j0, J // 2, "v_picked%d" % j0) for j0 in (0, J // 2)]
+        v_picked = sb([P, J], U32, "v_picked")
+        for j0, width in ((0, 256), (256, 256), (512, 512)):
+            nc.vector.tensor_copy(
+                v_picked[:, j0 : j0 + width],
+                v_words[:].bitcast(U32).indirect(offsets[:, j0 // STRIPE : (j0 + width) // STRIPE]),
+            )
         wi_q = quantise(interleave(wi_raw, "wi_bf", 1.0), "wi")
         wrd_q = quantise(interleave(wrd_raw, "wrd_bf", 1.0), "wrd")
         nwi_q = quantise(interleave(wi_raw, "nwi_bf", -1.0), "nwi")
@@ -130,32 +135,30 @@ def tile_list_cpxtab_dl_pow_kernel(
 
         def v_operand(s):
             j0 = s * SLICE
-            inner = j0 % (J // 2)
-            return v_picked[j0 // (J // 2)][:, inner : inner + SLICE], v_scales[:, j0 : j0 + SLICE]
+            return v_picked[:, j0 : j0 + SLICE], v_scales[:, j0 : j0 + SLICE]
 
-        for s in range(slices):
-            for m in range(N // M):
-                passes_e2m1(banks[s, m][:, :SLICE], m, *v_operand(s), start=True)
-        for s in range(slices):
-            for m in range(N // M):
-                pass_e4m3(banks[s, m][:, SLICE:], wi_q, m, *v_operand(s))
-        for s in range(slices):
-            for m in range(N // M):
-                pass_e4m3(banks[s, m][:, :SLICE], wrd_q, m, *v_operand(s))
-
+        v2_scales = gather(v2_plane[:], U8, 0, 2 * SLICE, "v2_scales")
         for s in range(slices):
             j0 = s * SLICE
-            scales = gather(v2_plane[:], U8, j0, SLICE, "v2_scales%d" % s, tag="v2_scales", bufs=2)
-            codes = gather(v2_words[:].bitcast(U32), U32, j0, SLICE, "v2_picked%d" % s, tag="v2_picked", bufs=2)
+            for m in range(N // M):
+                passes_e2m1(banks[s, m][:, :SLICE], m, *v_operand(s), start=True)
+            for m in range(N // M):
+                pass_e4m3(banks[s, m][:, SLICE:], wi_q, m, *v_operand(s))
+            for m in range(N // M):
+                pass_e4m3(banks[s, m][:, :SLICE], wrd_q, m, *v_operand(s))
+            scales = v2_scales[:, (s % 2) * SLICE : (s % 2 + 1) * SLICE]
+            if s >= 2:
+                nc.vector.tensor_copy(scales, v2_plane[:].indirect(offsets[:, j0 // STRIPE : (j0 + SLICE) // STRIPE]))
+            codes = gather(v2_words[:].bitcast(U32), U32, j0, SLICE, "v2_picked%d" % s, tag="v2_picked", bufs=3)
             for m in range(N // M):
                 bank = banks[s, m]
-                passes_e2m1(bank[:, SLICE:], m, codes[:], scales[:])
-                pass_e4m3(bank[:, SLICE:], wrd_q, m, codes[:], scales[:])
-                pass_e4m3(bank[:, :SLICE], nwi_q, m, codes[:], scales[:], stop=True)
+                passes_e2m1(bank[:, SLICE:], m, codes[:], scales)
+                pass_e4m3(bank[:, SLICE:], wrd_q, m, codes[:], scales)
+                pass_e4m3(bank[:, :SLICE], nwi_q, m, codes[:], scales, stop=True)
             for m in range(N // M):
                 squares = sb([P, 2 * SLICE], F32, "squares%d_%d" % (s, m))
                 nc.scalar.activation(squares[:], banks[s, m][:], ACT.Square)
                 power = sb([P, SLICE], F32, "power%d_%d" % (s, m))
-                adder = nc.vector if s == slices - 1 else nc.gpsimd
+                adder = nc.vector if s >= slices // 2 else nc.gpsimd
                 adder.tensor_tensor(power[:], squares[:, :SLICE], squares[:, SLICE:], ALU.add)
                 nc.sync.dma_start(out=out[m * M : (m + 1) * M, j0 : j0 + SLICE], in_=power[:])

@@ -31,7 +31,7 @@ def tile_list_cpxtab_dl_pow_kernel(
             return keep.tile(shape, dtype, name=name, align_bytes=64, **kw)
 
         def zero_plane(name, width):
-            plane = sb([P, width], U8, name)
+            plane = sb([P, width], U8, name, tag=name)
             nc.vector.memset(plane[:].bitcast(I32), 0)
             return plane
 
@@ -43,7 +43,7 @@ def tile_list_cpxtab_dl_pow_kernel(
                 )
 
         def load_words(words, name):
-            tile = sb([P, T], I32, name)
+            tile = sb([P, T], I32, name, tag=name)
             nc.sync.dma_start(out=tile[:], in_=words[0].rearrange("p t i -> p (t i)").bitcast(I32))
             return tile
 
@@ -129,6 +129,7 @@ def tile_list_cpxtab_dl_pow_kernel(
 
         slices = J // SLICE
         banks = {}
+        squares = {}
         for s in range(slices):
             for m in range(N // M):
                 banks[s, m] = psum.tile([P, 2 * SLICE], F32, name="bank%d_%d" % (s, m))
@@ -156,9 +157,17 @@ def tile_list_cpxtab_dl_pow_kernel(
                 pass_e4m3(bank[:, SLICE:], wrd_q, m, codes[:], scales)
                 pass_e4m3(bank[:, :SLICE], nwi_q, m, codes[:], scales, stop=True)
             for m in range(N // M):
-                squares = sb([P, 2 * SLICE], F32, "squares%d_%d" % (s, m))
-                nc.scalar.activation(squares[:], banks[s, m][:], ACT.Square)
-                power = sb([P, SLICE], F32, "power%d_%d" % (s, m))
-                adder = nc.vector if s >= slices // 2 else nc.gpsimd
-                adder.tensor_tensor(power[:], squares[:, :SLICE], squares[:, SLICE:], ALU.add)
-                nc.sync.dma_start(out=out[m * M : (m + 1) * M, j0 : j0 + SLICE], in_=power[:])
+                squares[s, m] = sb([P, 2 * SLICE], F32, "squares%d_%d" % (s, m))
+                nc.scalar.activation(squares[s, m][:], banks[s, m][:], ACT.Square)
+
+        out_rows = out.rearrange("(m p) j -> p m j", p=P)
+        for s in range(slices):
+            cols = slice(s * SLICE, (s + 1) * SLICE)
+            tag = ("v2_plane", "v2_words", "power2", "power3")[s]
+            power = sb([P, N // M, SLICE], F32, "power%d" % s, tag=tag)
+            for m in range(N // M):
+                nc.vector.tensor_tensor(power[:, m, :], squares[s, m][:, :SLICE], squares[s, m][:, SLICE:], ALU.add)
+                if s == slices - 1:
+                    nc.sync.dma_start(out=out_rows[:, m, cols], in_=power[:, m, :])
+            if s < slices - 1:
+                nc.sync.dma_start(out=out_rows[:, :, cols], in_=power[:])

@@ -13,10 +13,17 @@ ALU = mybir.AluOpType
 
 P = 128
 PACK = 4
-M = 128
-SLICE = 256
-HALF = 128
+QUADRANTS = 4
 STRIPE = 16
+M = 128
+ROW_TILES = N // M
+SLICE = 256
+SLICES = J // SLICE
+E2M1_N = 128
+RUN = 4
+V_WORD_RUNS = ((0, SLICE), (SLICE, SLICE), (2 * SLICE, 2 * SLICE))
+V2_WORD_RING = 3
+V2_SCALE_RING = 2
 
 
 def tile_list_cpxtab_dl_pow_kernel(
@@ -30,19 +37,19 @@ def tile_list_cpxtab_dl_pow_kernel(
         def sb(shape, dtype, name, **kw):
             return keep.tile(shape, dtype, name=name, align_bytes=64, **kw)
 
-        def zero_plane(name, width):
+        def zeroed_plane(name, width):
             plane = sb([P, width], U8, name, tag=name)
             nc.vector.memset(plane[:].bitcast(I32), 0)
             return plane
 
-        def load_plane(queue, plane, scales):
-            for q in range(4):
-                queue[q].dma_start(
-                    out=plane[32 * q : 32 * q + 4, :].bitcast(I32),
-                    in_=scales[0, 4 * q : 4 * q + 4, :].bitcast(I32),
+        def load_plane(queues, plane, scales):
+            for c in range(QUADRANTS):
+                queues[c].dma_start(
+                    out=plane[32 * c : 32 * c + 4, :].bitcast(I32),
+                    in_=scales[0, 4 * c : 4 * c + 4, :].bitcast(I32),
                 )
 
-        def load_words(words, name):
+        def load_table_words(words, name):
             tile = sb([P, T], I32, name, tag=name)
             nc.sync.dma_start(out=tile[:], in_=words[0].rearrange("p t i -> p (t i)").bitcast(I32))
             return tile
@@ -52,39 +59,34 @@ def tile_list_cpxtab_dl_pow_kernel(
             nc.sync.dma_start(out=raw[:], in_=w.rearrange("(p i) n -> p i n", i=PACK))
             return raw
 
-        v_plane = sb([P, T], U8, "v_plane")
-        nc.vector.memset(v_plane[:, : T // 2].bitcast(I32), 0)
-        nc.gpsimd.memset(v_plane[:, T // 2 :].bitcast(I32), 0)
+        tab_plane = zeroed_plane("tab_plane", T)
         offsets = keep.tile([P, J // STRIPE], U16, name="offsets")
         nc.sync.dma_start(offsets[:], offs)
-        wr4_plane = zero_plane("wr4_plane", N)
-        v2_plane = zero_plane("v2_plane", T)
+        wr4_plane = zeroed_plane("wr4_plane", N)
+        tab2_plane = zeroed_plane("tab2_plane", T)
         wr4_codes = sb([P, 2 * N], U8, "wr4_codes")
-        for m in range(N // M):
-            nc.sync.dma_start(out=wr4_codes[:, 2 * m * M : 2 * (m + 1) * M].bitcast(I32), in_=wr4_words[0, :, 2 * m * M : 2 * (m + 1) * M].bitcast(I32))
-        load_plane((nc.sync, nc.scalar, nc.sync, nc.scalar), v_plane, tab_scales)
-        v_words = load_words(tab_words, "v_words")
-        load_plane([nc.sync] * 4, wr4_plane, wr4_scales)
+        for m in range(ROW_TILES):
+            byte_cols = slice(2 * m * M, 2 * (m + 1) * M)
+            nc.sync.dma_start(out=wr4_codes[:, byte_cols].bitcast(I32), in_=wr4_words[0, :, byte_cols].bitcast(I32))
+        load_plane((nc.sync, nc.scalar, nc.sync, nc.scalar), tab_plane, tab_scales)
+        tab_codes = load_table_words(tab_words, "tab_codes")
+        load_plane([nc.sync] * QUADRANTS, wr4_plane, wr4_scales)
         wi_raw = load_weight(wi, "wi_raw")
         wrd_raw = load_weight(wrd, "wrd_raw")
-        load_plane([nc.sync] * 4, v2_plane, tab2_scales)
-        v2_words = load_words(tab2_words, "v2_words")
+        load_plane([nc.sync] * QUADRANTS, tab2_plane, tab2_scales)
+        tab2_codes = load_table_words(tab2_words, "tab2_codes")
 
-        def gather(window, dtype, j0, width, name, **kw):
-            picked = sb([P, width], dtype, name, **kw)
-            nc.vector.tensor_copy(
-                picked[:], window.indirect(offsets[:, j0 // STRIPE : (j0 + width) // STRIPE])
+        def gather(dst, window, j0, count):
+            nc.vector.tensor_copy(dst, window.indirect(offsets[:, j0 // STRIPE : (j0 + count) // STRIPE]))
+
+        def quantised(raw, name, sign):
+            grouped = sb([P, N, PACK], BF16, name + "_bf16")
+            nc.scalar.activation(
+                grouped[:].rearrange("p (c e) i -> p c i e", e=RUN),
+                raw[:].rearrange("p i (c e) -> p c i e", e=RUN),
+                ACT.Copy,
+                scale=sign,
             )
-            return picked
-
-        def interleave(raw, name, sign):
-            grouped = sb([P, N, PACK], BF16, name)
-            dst = grouped[:].rearrange("p (c e) i -> p c i e", e=4)
-            src = raw[:].rearrange("p i (c e) -> p c i e", e=4)
-            nc.scalar.activation(dst, src, ACT.Copy, scale=sign)
-            return grouped
-
-        def quantise(grouped, name):
             codes = sb([P, N], U32, name + "_codes")
             plane = sb([P, N], U8, name + "_plane")
             nc.vector.quantize_mx(
@@ -92,82 +94,89 @@ def tile_list_cpxtab_dl_pow_kernel(
             )
             return codes, plane
 
-        v_scales = gather(v_plane[:], U8, 0, J, "v_scales")
-        v_picked = sb([P, J], U32, "v_picked")
-        for j0, width in ((0, 256), (256, 256), (512, 512)):
-            nc.vector.tensor_copy(
-                v_picked[:, j0 : j0 + width],
-                v_words[:].bitcast(U32).indirect(offsets[:, j0 // STRIPE : (j0 + width) // STRIPE]),
-            )
-        wi_q = quantise(interleave(wi_raw, "wi_bf", 1.0), "wi")
-        wrd_q = quantise(interleave(wrd_raw, "wrd_bf", 1.0), "wrd")
-        nwi_q = quantise(interleave(wi_raw, "nwi_bf", -1.0), "nwi")
+        v_scales = sb([P, J], U8, "v_scales")
+        gather(v_scales[:], tab_plane[:], 0, J)
+        v_codes = sb([P, J], U32, "v_codes")
+        for j0, count in V_WORD_RUNS:
+            gather(v_codes[:, j0 : j0 + count], tab_codes[:].bitcast(U32), j0, count)
+        wi_q = quantised(wi_raw, "wi", 1.0)
+        wrd_q = quantised(wrd_raw, "wrd", 1.0)
+        minus_wi_q = quantised(wi_raw, "minus_wi", -1.0)
 
-        def pass_e4m3(dst, w, m, codes, scales, start=False, stop=False):
+        def e4m3_pass(dst, weight, m, moving, stop=False):
+            (w_codes, w_plane), (codes, scales) = weight, moving
             nc.tensor.matmul_mx(
                 out=dst,
-                lhsT=w[0][:, m * M : (m + 1) * M].bitcast(E4M3),
-                lhsT_scale=w[1][:, m * M : (m + 1) * M],
+                lhsT=w_codes[:, m * M : (m + 1) * M].bitcast(E4M3),
+                lhsT_scale=w_plane[:, m * M : (m + 1) * M],
                 rhs=codes.bitcast(E4M3),
                 rhs_scale=scales,
-                start=start,
+                start=False,
                 stop=stop,
             )
 
-        def passes_e2m1(dst, m, codes, scales, start=False, stop=False):
-            for h in range(SLICE // HALF):
-                cols = slice(h * HALF, (h + 1) * HALF)
+        def wr4_passes(dst, m, moving, start=False):
+            codes, scales = moving
+            for c0 in range(0, SLICE, E2M1_N):
+                cols = slice(c0, c0 + E2M1_N)
                 nc.tensor.matmul_mx(
                     out=dst[:, cols],
                     lhsT=wr4_codes[:, 2 * m * M : 2 * (m + 1) * M].bitcast(E2M1),
                     lhsT_scale=wr4_plane[:, m * M : (m + 1) * M],
                     rhs=codes[:, cols].bitcast(E4M3),
                     rhs_scale=scales[:, cols],
-                    start=start and h == 0,
-                    stop=stop and h == SLICE // HALF - 1,
+                    start=start and c0 == 0,
+                    stop=False,
                 )
 
-        slices = J // SLICE
         banks = {}
-        squares = {}
-        for s in range(slices):
-            for m in range(N // M):
+        for s in range(SLICES):
+            for m in range(ROW_TILES):
                 banks[s, m] = psum.tile([P, 2 * SLICE], F32, name="bank%d_%d" % (s, m))
+        squares = {}
 
-        def v_operand(s):
+        v2_scales = sb([P, V2_SCALE_RING * SLICE], U8, "v2_scales")
+        gather(v2_scales[:], tab2_plane[:], 0, V2_SCALE_RING * SLICE)
+        for s in range(SLICES):
             j0 = s * SLICE
-            return v_picked[:, j0 : j0 + SLICE], v_scales[:, j0 : j0 + SLICE]
+            zr = [banks[s, m][:, :SLICE] for m in range(ROW_TILES)]
+            zi = [banks[s, m][:, SLICE:] for m in range(ROW_TILES)]
+            v = (v_codes[:, j0 : j0 + SLICE], v_scales[:, j0 : j0 + SLICE])
+            for m in range(ROW_TILES):
+                wr4_passes(zr[m], m, v, start=True)
+            for m in range(ROW_TILES):
+                e4m3_pass(zi[m], wi_q, m, v)
+            wrd_v_ahead = s in (0, SLICES - 1)
+            if wrd_v_ahead:
+                for m in range(ROW_TILES):
+                    e4m3_pass(zr[m], wrd_q, m, v)
 
-        v2_scales = gather(v2_plane[:], U8, 0, 2 * SLICE, "v2_scales")
-        for s in range(slices):
-            j0 = s * SLICE
-            for m in range(N // M):
-                passes_e2m1(banks[s, m][:, :SLICE], m, *v_operand(s), start=True)
-            for m in range(N // M):
-                pass_e4m3(banks[s, m][:, SLICE:], wi_q, m, *v_operand(s))
-            for m in range(N // M):
-                pass_e4m3(banks[s, m][:, :SLICE], wrd_q, m, *v_operand(s))
-            scales = v2_scales[:, (s % 2) * SLICE : (s % 2 + 1) * SLICE]
-            if s >= 2:
-                nc.vector.tensor_copy(scales, v2_plane[:].indirect(offsets[:, j0 // STRIPE : (j0 + SLICE) // STRIPE]))
-            codes = gather(v2_words[:].bitcast(U32), U32, j0, SLICE, "v2_picked%d" % s, tag="v2_picked", bufs=3)
-            for m in range(N // M):
-                bank = banks[s, m]
-                passes_e2m1(bank[:, SLICE:], m, codes[:], scales)
-                pass_e4m3(bank[:, SLICE:], wrd_q, m, codes[:], scales)
-                pass_e4m3(bank[:, :SLICE], nwi_q, m, codes[:], scales, stop=True)
-            for m in range(N // M):
+            ring_col = (s % V2_SCALE_RING) * SLICE
+            v2_slice_scales = v2_scales[:, ring_col : ring_col + SLICE]
+            if s >= V2_SCALE_RING:
+                gather(v2_slice_scales, tab2_plane[:], j0, SLICE)
+            v2_codes = sb([P, SLICE], U32, "v2_codes%d" % s, tag="v2_codes", bufs=V2_WORD_RING)
+            gather(v2_codes[:], tab2_codes[:].bitcast(U32), j0, SLICE)
+            v2 = (v2_codes[:], v2_slice_scales)
+            for m in range(ROW_TILES):
+                wr4_passes(zi[m], m, v2)
+                e4m3_pass(zi[m], wrd_q, m, v2)
+                if not wrd_v_ahead:
+                    e4m3_pass(zr[m], wrd_q, m, v)
+                e4m3_pass(zr[m], minus_wi_q, m, v2, stop=True)
+            for m in range(ROW_TILES):
                 squares[s, m] = sb([P, 2 * SLICE], F32, "squares%d_%d" % (s, m))
                 nc.scalar.activation(squares[s, m][:], banks[s, m][:], ACT.Square)
 
         out_rows = out.rearrange("(m p) j -> p m j", p=P)
-        for s in range(slices):
+        result_tags = ("tab2_plane", "tab2_codes", "power2", "power3")
+        for s in range(SLICES):
             cols = slice(s * SLICE, (s + 1) * SLICE)
-            tag = ("v2_plane", "v2_words", "power2", "power3")[s]
-            power = sb([P, N // M, SLICE], F32, "power%d" % s, tag=tag)
-            for m in range(N // M):
+            last = s == SLICES - 1
+            power = sb([P, ROW_TILES, SLICE], F32, "power%d" % s, tag=result_tags[s])
+            for m in range(ROW_TILES):
                 nc.vector.tensor_tensor(power[:, m, :], squares[s, m][:, :SLICE], squares[s, m][:, SLICE:], ALU.add)
-                if s == slices - 1:
+                if last:
                     nc.sync.dma_start(out=out_rows[:, m, cols], in_=power[:, m, :])
-            if s < slices - 1:
+            if not last:
                 nc.sync.dma_start(out=out_rows[:, :, cols], in_=power[:])

@@ -19,11 +19,10 @@ M = 128
 ROW_TILES = N // M
 SLICE = 256
 SLICES = J // SLICE
+BANK, BANKS = 512, 8
 E2M1_N = 128
 RUN = 4
 V_WORD_RUNS = ((0, SLICE), (SLICE, SLICE), (2 * SLICE, 2 * SLICE))
-V2_WORD_RING = 3
-V2_SCALE_RING = 2
 
 
 def tile_list_cpxtab_dl_pow_kernel(
@@ -117,7 +116,7 @@ def tile_list_cpxtab_dl_pow_kernel(
 
         def wr4_passes(dst, m, moving, start=False):
             codes, scales = moving
-            for c0 in range(0, SLICE, E2M1_N):
+            for c0 in range(0, dst.shape[1], E2M1_N):
                 cols = slice(c0, c0 + E2M1_N)
                 nc.tensor.matmul_mx(
                     out=dst[:, cols],
@@ -129,54 +128,82 @@ def tile_list_cpxtab_dl_pow_kernel(
                     stop=False,
                 )
 
-        banks = {}
-        for s in range(SLICES):
-            for m in range(ROW_TILES):
-                banks[s, m] = psum.tile([P, 2 * SLICE], F32, name="bank%d_%d" % (s, m))
-        squares = {}
+        warm = psum.tile([P, BANK], F32, name="warm", tag="bank%d" % (BANKS - 1))
+        for c0 in (0, BANK):
+            nc.tensor.matmul_mx(
+                out=warm[:],
+                lhsT=wr4_codes[:, : 2 * M].bitcast(E2M1),
+                lhsT_scale=wr4_plane[:, :M],
+                rhs=tab_codes[:, c0 : c0 + BANK].bitcast(E4M3),
+                rhs_scale=tab_plane[:, c0 : c0 + BANK],
+                start=True,
+                stop=True,
+            )
 
-        v2_scales = sb([P, V2_SCALE_RING * SLICE], U8, "v2_scales")
-        gather(v2_scales[:], tab2_plane[:], 0, V2_SCALE_RING * SLICE)
+        early_scales = sb([P, 2 * SLICE], U8, "v2_scales")
+        gather(early_scales[:], tab2_plane[:], 0, 2 * SLICE)
+        early_codes = sb([P, 3 * SLICE], U32, "v2_codes")
+        squares = []
+        banks_used = 0
         for s in range(SLICES):
             j0 = s * SLICE
-            zr = [banks[s, m][:, :SLICE] for m in range(ROW_TILES)]
-            zi = [banks[s, m][:, SLICE:] for m in range(ROW_TILES)]
-            v = (v_codes[:, j0 : j0 + SLICE], v_scales[:, j0 : j0 + SLICE])
+            width = SLICE if s < SLICES - 1 else SLICE // 2
+            pieces = []
             for m in range(ROW_TILES):
-                wr4_passes(zr[m], m, v, start=True)
-            for m in range(ROW_TILES):
-                e4m3_pass(zi[m], wi_q, m, v)
-            wrd_v_ahead = s in (0, SLICES - 1)
-            if wrd_v_ahead:
-                for m in range(ROW_TILES):
-                    e4m3_pass(zr[m], wrd_q, m, v)
+                for c0 in range(0, SLICE, width):
+                    bank = psum.tile([P, BANK], F32, name="bank%d" % banks_used, tag="bank%d" % (banks_used % BANKS))
+                    pieces.append((m, slice(c0, c0 + width), bank[:, :width], bank[:, width : 2 * width], bank[:, : 2 * width]))
+                    banks_used = banks_used + 1
 
-            ring_col = (s % V2_SCALE_RING) * SLICE
-            v2_slice_scales = v2_scales[:, ring_col : ring_col + SLICE]
-            if s >= V2_SCALE_RING:
-                gather(v2_slice_scales, tab2_plane[:], j0, SLICE)
-            v2_codes = sb([P, SLICE], U32, "v2_codes%d" % s, tag="v2_codes", bufs=V2_WORD_RING)
-            gather(v2_codes[:], tab2_codes[:].bitcast(U32), j0, SLICE)
-            v2 = (v2_codes[:], v2_slice_scales)
-            for m in range(ROW_TILES):
-                wr4_passes(zi[m], m, v2)
-                e4m3_pass(zi[m], wrd_q, m, v2)
-                if not wrd_v_ahead:
-                    e4m3_pass(zr[m], wrd_q, m, v)
-                e4m3_pass(zr[m], minus_wi_q, m, v2, stop=True)
-            for m in range(ROW_TILES):
-                squares[s, m] = sb([P, 2 * SLICE], F32, "squares%d_%d" % (s, m))
-                nc.scalar.activation(squares[s, m][:], banks[s, m][:], ACT.Square)
+            v_slice_codes, v_slice_scales = v_codes[:, j0 : j0 + SLICE], v_scales[:, j0 : j0 + SLICE]
+            for m, cols, zr, zi, both in pieces:
+                wr4_passes(zr, m, (v_slice_codes[:, cols], v_slice_scales[:, cols]), start=True)
+            for m, cols, zr, zi, both in pieces:
+                e4m3_pass(zi, wi_q, m, (v_slice_codes[:, cols], v_slice_scales[:, cols]))
+            behind = (1,) if s < 2 else ()
+            for m, cols, zr, zi, both in pieces:
+                if m not in behind:
+                    e4m3_pass(zr, wrd_q, m, (v_slice_codes[:, cols], v_slice_scales[:, cols]))
+
+            if s < 2:
+                v2_scales = early_scales[:, j0 : j0 + SLICE]
+            else:
+                v2_scales = v_scales[:, j0 - 2 * SLICE : j0 - SLICE]
+                gather(v2_scales, tab2_plane[:], j0, SLICE)
+            v2_codes = early_codes[:, j0 : j0 + SLICE] if s < 3 else v_codes[:, :SLICE]
+            gather(v2_codes, tab2_codes[:].bitcast(U32), j0, SLICE)
+            for m, cols, zr, zi, both in pieces:
+                v2 = (v2_codes[:, cols], v2_scales[:, cols])
+                wr4_passes(zi, m, v2)
+                if m in behind:
+                    e4m3_pass(zr, wrd_q, m, (v_slice_codes[:, cols], v_slice_scales[:, cols]))
+                e4m3_pass(zi, wrd_q, m, v2)
+                e4m3_pass(zr, minus_wi_q, m, v2, stop=True)
+            slice_squares = sb([P, len(pieces), 2, width], F32, "squares%d" % s)
+            squares.append(slice_squares)
+            for i, (m, cols, zr, zi, both) in enumerate(pieces):
+                nc.scalar.activation(slice_squares[:, i].rearrange("p z j -> p (z j)"), both, ACT.Square)
 
         out_rows = out.rearrange("(m p) j -> p m j", p=P)
-        result_tags = ("tab2_plane", "tab2_codes", "power2", "power3")
-        for s in range(SLICES):
-            cols = slice(s * SLICE, (s + 1) * SLICE)
-            last = s == SLICES - 1
-            power = sb([P, ROW_TILES, SLICE], F32, "power%d" % s, tag=result_tags[s])
-            for m in range(ROW_TILES):
-                nc.vector.tensor_tensor(power[:, m, :], squares[s, m][:, :SLICE], squares[s, m][:, SLICE:], ALU.add)
-                if last:
-                    nc.sync.dma_start(out=out_rows[:, m, cols], in_=power[:, m, :])
-            if not last:
-                nc.sync.dma_start(out=out_rows[:, :, cols], in_=power[:])
+        power = [
+            sb([P, ROW_TILES, SLICE], F32, "power%d" % s, tag=tag)
+            for s, tag in enumerate(("power0", "tab2_codes", "tab2_plane", "power3"))
+        ]
+        nc.gpsimd.tensor_tensor(power[0][:], squares[0][:, :, 0, :], squares[0][:, :, 1, :], ALU.add)
+        nc.sync.dma_start(out=out_rows[:, :, :SLICE], in_=power[0][:])
+        nc.vector.tensor_tensor(power[1][:], squares[1][:, :, 0, :], squares[1][:, :, 1, :], ALU.add)
+        nc.sync.dma_start(out=out_rows[:, :, SLICE : 2 * SLICE], in_=power[1][:])
+        for m in range(ROW_TILES):
+            nc.vector.tensor_tensor(power[2][:, m, :], squares[2][:, m, 0, :], squares[2][:, m, 1, :], ALU.add)
+        nc.sync.dma_start(out=out_rows[:, :, 2 * SLICE : 3 * SLICE], in_=power[2][:])
+        half = SLICE // 2
+        for m in range(ROW_TILES):
+            for h in range(2):
+                cols = slice(h * half, (h + 1) * half)
+                piece = squares[3][:, 2 * m + h]
+                nc.vector.tensor_tensor(power[3][:, m, cols], piece[:, 0, :], piece[:, 1, :], ALU.add)
+                if m == ROW_TILES - 1:
+                    j0 = 3 * SLICE + h * half
+                    nc.sync.dma_start(out=out_rows[:, m, j0 : j0 + half], in_=power[3][:, m, cols])
+            if m < ROW_TILES - 1:
+                nc.sync.dma_start(out=out_rows[:, m, 3 * SLICE :], in_=power[3][:, m, :])

@@ -14,12 +14,14 @@ ALU = mybir.AluOpType
 P = 128
 PACK = 4
 QUADRANTS = 4
+ROWS = 4
 STRIPE = 16
 M = 128
 ROW_TILES = N // M
 SLICE = 256
 SLICES = J // SLICE
 BANK, BANKS = 512, 8
+GPSIMD_PIECES = 3
 E2M1_N = 128
 RUN = 4
 V_WORD_RUNS = ((0, SLICE), (SLICE, SLICE), (2 * SLICE, 2 * SLICE))
@@ -42,10 +44,10 @@ def tile_list_cpxtab_dl_pow_kernel(
             return plane
 
         def load_plane(queues, plane, scales):
-            for c in range(QUADRANTS):
-                queues[c].dma_start(
-                    out=plane[32 * c : 32 * c + 4, :].bitcast(I32),
-                    in_=scales[0, 4 * c : 4 * c + 4, :].bitcast(I32),
+            for r in range(ROWS):
+                queues[r].dma_start(
+                    out=plane[r:P:32, :].bitcast(I32),
+                    in_=scales[0, r : QUADRANTS * ROWS : ROWS, :].bitcast(I32),
                 )
 
         def load_table_words(words, name):
@@ -69,10 +71,10 @@ def tile_list_cpxtab_dl_pow_kernel(
             nc.sync.dma_start(out=wr4_codes[:, byte_cols].bitcast(I32), in_=wr4_words[0, :, byte_cols].bitcast(I32))
         load_plane((nc.sync, nc.scalar, nc.sync, nc.scalar), tab_plane, tab_scales)
         tab_codes = load_table_words(tab_words, "tab_codes")
-        load_plane([nc.sync] * QUADRANTS, wr4_plane, wr4_scales)
+        load_plane([nc.sync] * ROWS, wr4_plane, wr4_scales)
         wi_raw = load_weight(wi, "wi_raw")
         wrd_raw = load_weight(wrd, "wrd_raw")
-        load_plane([nc.sync] * QUADRANTS, tab2_plane, tab2_scales)
+        load_plane([nc.sync] * ROWS, tab2_plane, tab2_scales)
         tab2_codes = load_table_words(tab2_words, "tab2_codes")
 
         def gather(dst, window, j0, count):
@@ -185,25 +187,23 @@ def tile_list_cpxtab_dl_pow_kernel(
                 nc.scalar.activation(slice_squares[:, i].rearrange("p z j -> p (z j)"), both, ACT.Square)
 
         out_rows = out.rearrange("(m p) j -> p m j", p=P)
-        power = [
-            sb([P, ROW_TILES, SLICE], F32, "power%d" % s, tag=tag)
-            for s, tag in enumerate(("power0", "tab2_codes", "tab2_plane", "power3"))
-        ]
-        nc.gpsimd.tensor_tensor(power[0][:], squares[0][:, :, 0, :], squares[0][:, :, 1, :], ALU.add)
-        nc.sync.dma_start(out=out_rows[:, :, :SLICE], in_=power[0][:])
-        nc.vector.tensor_tensor(power[1][:], squares[1][:, :, 0, :], squares[1][:, :, 1, :], ALU.add)
-        nc.sync.dma_start(out=out_rows[:, :, SLICE : 2 * SLICE], in_=power[1][:])
-        for m in range(ROW_TILES):
-            nc.vector.tensor_tensor(power[2][:, m, :], squares[2][:, m, 0, :], squares[2][:, m, 1, :], ALU.add)
-        nc.sync.dma_start(out=out_rows[:, :, 2 * SLICE : 3 * SLICE], in_=power[2][:])
+        held_behind = {(1, 1): "tab2_plane", (2, 0): "tab2_codes"}
+        for s in range(SLICES - 1):
+            for m in range(ROW_TILES):
+                adder = nc.gpsimd if s * ROW_TILES + m < GPSIMD_PIECES else nc.vector
+                name = "power%d_%d" % (s, m)
+                power = sb([P, SLICE], F32, name, tag=held_behind.get((s, m), name))
+                adder.tensor_tensor(power[:], squares[s][:, m, 0, :], squares[s][:, m, 1, :], ALU.add)
+                nc.sync.dma_start(out=out_rows[:, m, s * SLICE : (s + 1) * SLICE], in_=power[:])
         half = SLICE // 2
+        power = sb([P, ROW_TILES, SLICE], F32, "power_last")
         for m in range(ROW_TILES):
             for h in range(2):
                 cols = slice(h * half, (h + 1) * half)
-                piece = squares[3][:, 2 * m + h]
-                nc.vector.tensor_tensor(power[3][:, m, cols], piece[:, 0, :], piece[:, 1, :], ALU.add)
+                piece = squares[SLICES - 1][:, 2 * m + h]
+                nc.vector.tensor_tensor(power[:, m, cols], piece[:, 0, :], piece[:, 1, :], ALU.add)
                 if m == ROW_TILES - 1:
-                    j0 = 3 * SLICE + h * half
-                    nc.sync.dma_start(out=out_rows[:, m, j0 : j0 + half], in_=power[3][:, m, cols])
+                    j0 = J - SLICE + h * half
+                    nc.sync.dma_start(out=out_rows[:, m, j0 : j0 + half], in_=power[:, m, cols])
             if m < ROW_TILES - 1:
-                nc.sync.dma_start(out=out_rows[:, m, 3 * SLICE :], in_=power[3][:, m, :])
+                nc.sync.dma_start(out=out_rows[:, m, J - SLICE :], in_=power[:, m, :])

@@ -24,7 +24,6 @@ BANK, BANKS = 512, 8
 GPSIMD_PIECES = 3
 E2M1_N = 128
 RUN = 4
-V_WORD_RUNS = ((0, SLICE), (SLICE, SLICE), (2 * SLICE, 2 * SLICE))
 
 
 def tile_list_cpxtab_dl_pow_kernel(
@@ -98,8 +97,8 @@ def tile_list_cpxtab_dl_pow_kernel(
         v_scales = sb([P, J], U8, "v_scales")
         gather(v_scales[:], tab_plane[:], 0, J)
         v_codes = sb([P, J], U32, "v_codes")
-        for j0, count in V_WORD_RUNS:
-            gather(v_codes[:, j0 : j0 + count], tab_codes[:].bitcast(U32), j0, count)
+        for j0 in range(0, J, SLICE):
+            gather(v_codes[:, j0 : j0 + SLICE], tab_codes[:].bitcast(U32), j0, SLICE)
         wi_q = quantised(wi_raw, "wi", 1.0)
         wrd_q = quantised(wrd_raw, "wrd", 1.0)
         minus_wi_q = quantised(wi_raw, "minus_wi", -1.0)
@@ -129,18 +128,6 @@ def tile_list_cpxtab_dl_pow_kernel(
                     start=start and c0 == 0,
                     stop=False,
                 )
-
-        warm = psum.tile([P, BANK], F32, name="warm", tag="bank%d" % (BANKS - 1))
-        for c0 in (0, BANK):
-            nc.tensor.matmul_mx(
-                out=warm[:],
-                lhsT=wr4_codes[:, : 2 * M].bitcast(E2M1),
-                lhsT_scale=wr4_plane[:, :M],
-                rhs=tab_codes[:, c0 : c0 + BANK].bitcast(E4M3),
-                rhs_scale=tab_plane[:, c0 : c0 + BANK],
-                start=True,
-                stop=True,
-            )
 
         early_scales = sb([P, 2 * SLICE], U8, "v2_scales")
         gather(early_scales[:], tab2_plane[:], 0, 2 * SLICE)

@@ -65,9 +65,7 @@ def tile_list_cpxtab_dl_pow_kernel(
         wr4_plane = zeroed_plane("wr4_plane", N)
         tab2_plane = zeroed_plane("tab2_plane", T)
         wr4_codes = sb([P, 2 * N], U8, "wr4_codes")
-        for m in range(ROW_TILES):
-            byte_cols = slice(2 * m * M, 2 * (m + 1) * M)
-            nc.sync.dma_start(out=wr4_codes[:, byte_cols].bitcast(I32), in_=wr4_words[0, :, byte_cols].bitcast(I32))
+        nc.sync.dma_start(out=wr4_codes[:].bitcast(I32), in_=wr4_words[0].bitcast(I32))
         load_plane((nc.sync, nc.scalar, nc.sync, nc.scalar), tab_plane, tab_scales)
         tab_codes = load_table_words(tab_words, "tab_codes")
         load_plane([nc.sync] * ROWS, wr4_plane, wr4_scales)
@@ -79,14 +77,16 @@ def tile_list_cpxtab_dl_pow_kernel(
         def gather(dst, window, j0, count):
             nc.vector.tensor_copy(dst, window.indirect(offsets[:, j0 // STRIPE : (j0 + count) // STRIPE]))
 
-        def quantised(raw, name, sign):
+        def rounded(raw, name):
             grouped = sb([P, N, PACK], BF16, name + "_bf16")
             nc.scalar.activation(
                 grouped[:].rearrange("p (c e) i -> p c i e", e=RUN),
                 raw[:].rearrange("p i (c e) -> p c i e", e=RUN),
                 ACT.Copy,
-                scale=sign,
             )
+            return grouped
+
+        def quantised(grouped, name):
             codes = sb([P, N], U32, name + "_codes")
             plane = sb([P, N], U8, name + "_plane")
             nc.vector.quantize_mx(
@@ -99,9 +99,13 @@ def tile_list_cpxtab_dl_pow_kernel(
         v_codes = sb([P, J], U32, "v_codes")
         for j0 in range(0, J, SLICE):
             gather(v_codes[:, j0 : j0 + SLICE], tab_codes[:].bitcast(U32), j0, SLICE)
-        wi_q = quantised(wi_raw, "wi", 1.0)
-        wrd_q = quantised(wrd_raw, "wrd", 1.0)
-        minus_wi_q = quantised(wi_raw, "minus_wi", -1.0)
+        wi_bf16 = rounded(wi_raw, "wi")
+        wi_q = quantised(wi_bf16, "wi")
+        wrd_q = quantised(rounded(wrd_raw, "wrd"), "wrd")
+        first, second = (wi_bf16[:, m * M : (m + 1) * M, :].rearrange("p n i -> p (n i)") for m in range(ROW_TILES))
+        nc.gpsimd.tensor_scalar(first, first, -1.0, 0.0, ALU.mult, ALU.add)
+        nc.scalar.activation(second, second, ACT.Copy, scale=-1.0)
+        minus_wi_q = quantised(wi_bf16, "minus_wi")
 
         def e4m3_pass(dst, weight, m, moving, stop=False):
             (w_codes, w_plane), (codes, scales) = weight, moving

@@ -65,7 +65,9 @@ def tile_list_cpxtab_dl_pow_kernel(
         wr4_plane = zeroed_plane("wr4_plane", N)
         tab2_plane = zeroed_plane("tab2_plane", T)
         wr4_codes = sb([P, 2 * N], U8, "wr4_codes")
-        nc.sync.dma_start(out=wr4_codes[:].bitcast(I32), in_=wr4_words[0].bitcast(I32))
+        for m in range(ROW_TILES):
+            byte_cols = slice(2 * m * M, 2 * (m + 1) * M)
+            nc.sync.dma_start(out=wr4_codes[:, byte_cols].bitcast(I32), in_=wr4_words[0, :, byte_cols].bitcast(I32))
         load_plane((nc.sync, nc.scalar, nc.sync, nc.scalar), tab_plane, tab_scales)
         tab_codes = load_table_words(tab_words, "tab_codes")
         load_plane([nc.sync] * ROWS, wr4_plane, wr4_scales)

@@ -65,10 +65,8 @@ def tile_list_cpxtab_dl_pow_kernel(
         wr4_plane = zeroed_plane("wr4_plane", N)
         tab2_plane = zeroed_plane("tab2_plane", T)
         wr4_codes = sb([P, 2 * N], U8, "wr4_codes")
-        for m in range(ROW_TILES):
-            byte_cols = slice(2 * m * M, 2 * (m + 1) * M)
-            nc.sync.dma_start(out=wr4_codes[:, byte_cols].bitcast(I32), in_=wr4_words[0, :, byte_cols].bitcast(I32))
-        load_plane((nc.sync, nc.scalar, nc.sync, nc.scalar), tab_plane, tab_scales)
+        nc.sync.dma_start(out=wr4_codes[:].bitcast(I32), in_=wr4_words[0].bitcast(I32))
+        load_plane([nc.sync] * ROWS, tab_plane, tab_scales)
         tab_codes = load_table_words(tab_words, "tab_codes")
         load_plane([nc.sync] * ROWS, wr4_plane, wr4_scales)
         wi_raw = load_weight(wi, "wi_raw")

@@ -13,16 +13,19 @@ ALU = mybir.AluOpType
 
 P = 128
 PACK = 4
-QUADRANTS = 4
+QUADRANT = 32
 ROWS = 4
+BLOCKS = K // 32
 STRIPE = 16
 M = 128
 ROW_TILES = N // M
 SLICE = 256
 SLICES = J // SLICE
+LAST = SLICES - 1
 BANK, BANKS = 512, 8
 GPSIMD_PIECES = 3
 E2M1_N = 128
+HEAD = T // 4
 RUN = 4
 
 
@@ -42,43 +45,43 @@ def tile_list_cpxtab_dl_pow_kernel(
             nc.vector.memset(plane[:].bitcast(I32), 0)
             return plane
 
-        def load_plane(queues, plane, scales):
+        def fill_plane(queues, plane, rows):
             for r in range(ROWS):
-                queues[r].dma_start(
-                    out=plane[r:P:32, :].bitcast(I32),
-                    in_=scales[0, r : QUADRANTS * ROWS : ROWS, :].bitcast(I32),
-                )
+                queues[r].dma_start(out=plane[r:P:QUADRANT, :].bitcast(I32), in_=rows[r:BLOCKS:ROWS, :].bitcast(I32))
 
-        def load_table_words(words, name):
-            tile = sb([P, T], I32, name, tag=name)
-            nc.sync.dma_start(out=tile[:], in_=words[0].rearrange("p t i -> p (t i)").bitcast(I32))
-            return tile
+        def load_words(tile, words, cols):
+            nc.sync.dma_start(out=tile[:, cols], in_=words[0].rearrange("p t i -> p (t i)").bitcast(I32)[:, cols])
 
-        def load_weight(w, name):
-            raw = sb([P, PACK, N], F32, name)
+        def load_weight(raw, w):
             nc.sync.dma_start(out=raw[:], in_=w.rearrange("(p i) n -> p i n", i=PACK))
-            return raw
 
-        tab_plane = zeroed_plane("tab_plane", T)
         offsets = keep.tile([P, J // STRIPE], U16, name="offsets")
         nc.sync.dma_start(offsets[:], offs)
+        tab2_rows = sb([P, T], U8, "tab2_rows")
+        nc.sync.dma_start(out=tab2_rows[P - BLOCKS :, :].bitcast(I32), in_=tab2_scales[0].bitcast(I32))
+        tab_plane = zeroed_plane("tab_plane", T)
         wr4_plane = zeroed_plane("wr4_plane", N)
-        tab2_plane = zeroed_plane("tab2_plane", T)
+        nc.vector.memset(tab2_rows[: P - BLOCKS, :].bitcast(I32), 0)
+        v2_scales = zeroed_plane("v2_scales", J)
+        tab_codes = sb([P, T], I32, "tab_codes", tag="tab_codes")
+        load_words(tab_codes, tab_words, slice(0, HEAD))
+        fill_plane([nc.sync] * ROWS, tab_plane, tab_scales[0])
+        load_words(tab_codes, tab_words, slice(HEAD, T))
+        wi_raw = sb([P, PACK, N], F32, "wi_raw", tag="wi_raw")
+        load_weight(wi_raw, wi)
         wr4_codes = sb([P, 2 * N], U8, "wr4_codes")
         nc.sync.dma_start(out=wr4_codes[:].bitcast(I32), in_=wr4_words[0].bitcast(I32))
-        load_plane([nc.sync] * ROWS, tab_plane, tab_scales)
-        tab_codes = load_table_words(tab_words, "tab_codes")
-        load_plane([nc.sync] * ROWS, wr4_plane, wr4_scales)
-        wi_raw = load_weight(wi, "wi_raw")
-        wrd_raw = load_weight(wrd, "wrd_raw")
-        load_plane([nc.sync] * ROWS, tab2_plane, tab2_scales)
-        tab2_codes = load_table_words(tab2_words, "tab2_codes")
+        fill_plane([nc.sync] * ROWS, wr4_plane, wr4_scales[0])
+        wrd_raw = sb([P, PACK, N], F32, "wrd_raw", tag="wrd_raw")
+        load_weight(wrd_raw, wrd)
+        tab2_codes = sb([P, T], I32, "tab2_codes")
+        load_words(tab2_codes, tab2_words, slice(0, T))
 
         def gather(dst, window, j0, count):
             nc.vector.tensor_copy(dst, window.indirect(offsets[:, j0 // STRIPE : (j0 + count) // STRIPE]))
 
         def rounded(raw, name):
-            grouped = sb([P, N, PACK], BF16, name + "_bf16")
+            grouped = sb([P, N, PACK], BF16, name + "_bf16", tag=name + "_bf16")
             nc.scalar.activation(
                 grouped[:].rearrange("p (c e) i -> p c i e", e=RUN),
                 raw[:].rearrange("p i (c e) -> p c i e", e=RUN),
@@ -94,92 +97,112 @@ def tile_list_cpxtab_dl_pow_kernel(
             )
             return codes, plane
 
-        v_scales = sb([P, J], U8, "v_scales")
-        gather(v_scales[:], tab_plane[:], 0, J)
-        v_codes = sb([P, J], U32, "v_codes")
-        for j0 in range(0, J, SLICE):
+        v2_rows = sb([P, J], U8, "v2_rows")
+        gather(v2_rows[:], tab2_rows[:], 0, J)
+        fill_plane([nc.sync] * ROWS, v2_scales, v2_rows[P - BLOCKS :, :])
+
+        def gather_v(s, codes, scales):
+            gather(codes, tab_codes[:].bitcast(U32), s * SLICE, SLICE)
+            gather(scales, tab_plane[:], s * SLICE, SLICE)
+            return codes, scales
+
+        v = []
+        early_scales = sb([P, 2 * SLICE], U8, "v_scales")
+        gather(early_scales[:], tab_plane[:], 0, 2 * SLICE)
+        v_codes = sb([P, LAST * SLICE], U32, "v_codes")
+        for j0 in range(0, LAST * SLICE, SLICE):
             gather(v_codes[:, j0 : j0 + SLICE], tab_codes[:].bitcast(U32), j0, SLICE)
+        for j0 in range(0, 2 * SLICE, SLICE):
+            v.append((v_codes[:, j0 : j0 + SLICE], early_scales[:, j0 : j0 + SLICE]))
         wi_bf16 = rounded(wi_raw, "wi")
         wi_q = quantised(wi_bf16, "wi")
+        third_scales = sb([P, SLICE], U8, "v_scales2", tag="wi_raw")
+        gather(third_scales[:], tab_plane[:], 2 * SLICE, SLICE)
+        v.append((v_codes[:, 2 * SLICE :], third_scales[:]))
         wrd_q = quantised(rounded(wrd_raw, "wrd"), "wrd")
-        first, second = (wi_bf16[:, m * M : (m + 1) * M, :].rearrange("p n i -> p (n i)") for m in range(ROW_TILES))
-        nc.gpsimd.tensor_scalar(first, first, -1.0, 0.0, ALU.mult, ALU.add)
-        nc.scalar.activation(second, second, ACT.Copy, scale=-1.0)
-        minus_wi_q = quantised(wi_bf16, "minus_wi")
+        minus_wi_bf16 = sb([P, N, PACK], BF16, "minus_wi_bf16", tag="wrd_raw")
+        nc.scalar.activation(
+            minus_wi_bf16[:].rearrange("p n i -> p (n i)"), wi_bf16[:].rearrange("p n i -> p (n i)"), ACT.Copy, scale=-1.0
+        )
+        first_codes = sb([P, SLICE], U32, "v2_codes0", tag="wrd_bf16")
+        gather(first_codes[:], tab2_codes[:].bitcast(U32), 0, SLICE)
+        minus_wi_q = quantised(minus_wi_bf16, "minus_wi")
+        later_codes = sb([P, LAST * SLICE], U32, "v2_codes", tag="wrd_raw")
 
-        def e4m3_pass(dst, weight, m, moving, stop=False):
+        def e4m3_pass(dst, weight, m, moving, cols, stop=False):
             (w_codes, w_plane), (codes, scales) = weight, moving
             nc.tensor.matmul_mx(
                 out=dst,
                 lhsT=w_codes[:, m * M : (m + 1) * M].bitcast(E4M3),
                 lhsT_scale=w_plane[:, m * M : (m + 1) * M],
-                rhs=codes.bitcast(E4M3),
-                rhs_scale=scales,
+                rhs=codes[:, cols].bitcast(E4M3),
+                rhs_scale=scales[:, cols],
                 start=False,
                 stop=stop,
             )
 
-        def wr4_passes(dst, m, moving, start=False):
+        def wr4_passes(dst, m, moving, cols, start=False):
             codes, scales = moving
             for c0 in range(0, dst.shape[1], E2M1_N):
-                cols = slice(c0, c0 + E2M1_N)
+                part = slice(cols.start + c0, cols.start + c0 + E2M1_N)
                 nc.tensor.matmul_mx(
-                    out=dst[:, cols],
+                    out=dst[:, c0 : c0 + E2M1_N],
                     lhsT=wr4_codes[:, 2 * m * M : 2 * (m + 1) * M].bitcast(E2M1),
                     lhsT_scale=wr4_plane[:, m * M : (m + 1) * M],
-                    rhs=codes[:, cols].bitcast(E4M3),
-                    rhs_scale=scales[:, cols],
+                    rhs=codes[:, part].bitcast(E4M3),
+                    rhs_scale=scales[:, part],
                     start=start and c0 == 0,
                     stop=False,
                 )
 
-        early_scales = sb([P, 2 * SLICE], U8, "v2_scales")
-        gather(early_scales[:], tab2_plane[:], 0, 2 * SLICE)
-        early_codes = sb([P, 3 * SLICE], U32, "v2_codes")
         squares = []
         banks_used = 0
         for s in range(SLICES):
             j0 = s * SLICE
-            width = SLICE if s < SLICES - 1 else SLICE // 2
+            width = SLICE if s < LAST else SLICE // 2
             pieces = []
             for m in range(ROW_TILES):
                 for c0 in range(0, SLICE, width):
                     bank = psum.tile([P, BANK], F32, name="bank%d" % banks_used, tag="bank%d" % (banks_used % BANKS))
                     pieces.append((m, slice(c0, c0 + width), bank[:, :width], bank[:, width : 2 * width], bank[:, : 2 * width]))
                     banks_used = banks_used + 1
-
-            v_slice_codes, v_slice_scales = v_codes[:, j0 : j0 + SLICE], v_scales[:, j0 : j0 + SLICE]
-            for m, cols, zr, zi, both in pieces:
-                wr4_passes(zr, m, (v_slice_codes[:, cols], v_slice_scales[:, cols]), start=True)
-            for m, cols, zr, zi, both in pieces:
-                e4m3_pass(zi, wi_q, m, (v_slice_codes[:, cols], v_slice_scales[:, cols]))
-            behind = (1,) if s < 2 else ()
-            for m, cols, zr, zi, both in pieces:
-                if m not in behind:
-                    e4m3_pass(zr, wrd_q, m, (v_slice_codes[:, cols], v_slice_scales[:, cols]))
-
-            if s < 2:
-                v2_scales = early_scales[:, j0 : j0 + SLICE]
+            v2 = (later_codes[:, j0 - SLICE : j0] if s else first_codes[:], v2_scales[:, j0 : j0 + SLICE])
+            if s < LAST:
+                for m, cols, zr, zi, both in pieces:
+                    wr4_passes(zr, m, v[s], cols, start=True)
+                for m, cols, zr, zi, both in pieces:
+                    e4m3_pass(zi, wi_q, m, v[s], cols)
+                behind = (1,) if s == 0 else ()
+                for m, cols, zr, zi, both in pieces:
+                    if m not in behind:
+                        e4m3_pass(zr, wrd_q, m, v[s], cols)
+                if s:
+                    gather(v2[0], tab2_codes[:].bitcast(U32), j0, SLICE)
+                for m, cols, zr, zi, both in pieces:
+                    wr4_passes(zi, m, v2, cols)
+                    if m in behind:
+                        e4m3_pass(zr, wrd_q, m, v[s], cols)
+                    e4m3_pass(zi, wrd_q, m, v2, cols)
+                    e4m3_pass(zr, minus_wi_q, m, v2, cols, stop=True)
             else:
-                v2_scales = v_scales[:, j0 - 2 * SLICE : j0 - SLICE]
-                gather(v2_scales, tab2_plane[:], j0, SLICE)
-            v2_codes = early_codes[:, j0 : j0 + SLICE] if s < 3 else v_codes[:, :SLICE]
-            gather(v2_codes, tab2_codes[:].bitcast(U32), j0, SLICE)
-            for m, cols, zr, zi, both in pieces:
-                v2 = (v2_codes[:, cols], v2_scales[:, cols])
-                wr4_passes(zi, m, v2)
-                if m in behind:
-                    e4m3_pass(zr, wrd_q, m, (v_slice_codes[:, cols], v_slice_scales[:, cols]))
-                e4m3_pass(zi, wrd_q, m, v2)
-                e4m3_pass(zr, minus_wi_q, m, v2, stop=True)
+                gather(v2[0], tab2_codes[:].bitcast(U32), j0, SLICE)
+                for m, cols, zr, zi, both in pieces:
+                    wr4_passes(zi, m, v2, cols, start=True)
+                    e4m3_pass(zi, wrd_q, m, v2, cols)
+                    e4m3_pass(zr, minus_wi_q, m, v2, cols)
+                last_v = gather_v(s, v[0][0], v[0][1])
+                for m, cols, zr, zi, both in pieces:
+                    wr4_passes(zr, m, last_v, cols)
+                    e4m3_pass(zr, wrd_q, m, last_v, cols)
+                    e4m3_pass(zi, wi_q, m, last_v, cols, stop=True)
             slice_squares = sb([P, len(pieces), 2, width], F32, "squares%d" % s)
             squares.append(slice_squares)
             for i, (m, cols, zr, zi, both) in enumerate(pieces):
                 nc.scalar.activation(slice_squares[:, i].rearrange("p z j -> p (z j)"), both, ACT.Square)
 
         out_rows = out.rearrange("(m p) j -> p m j", p=P)
-        held_behind = {(1, 1): "tab2_plane", (2, 0): "tab2_codes"}
-        for s in range(SLICES - 1):
+        held_behind = {(1, 1): "tab_plane", (2, 0): "tab_codes"}
+        for s in range(LAST):
             for m in range(ROW_TILES):
                 adder = nc.gpsimd if s * ROW_TILES + m < GPSIMD_PIECES else nc.vector
                 name = "power%d_%d" % (s, m)
@@ -191,7 +214,7 @@ def tile_list_cpxtab_dl_pow_kernel(
         for m in range(ROW_TILES):
             for h in range(2):
                 cols = slice(h * half, (h + 1) * half)
-                piece = squares[SLICES - 1][:, 2 * m + h]
+                piece = squares[LAST][:, 2 * m + h]
                 nc.vector.tensor_tensor(power[:, m, cols], piece[:, 0, :], piece[:, 1, :], ALU.add)
                 if m == ROW_TILES - 1:
                     j0 = J - SLICE + h * half

@@ -26,6 +26,7 @@ BANK, BANKS = 512, 8
 GPSIMD_PIECES = 3
 E2M1_N = 128
 HEAD = T // 4
+WRD_AT, TAB_AT = 0, 4 * N * PACK
 RUN = 4
 
 
@@ -35,10 +36,14 @@ def tile_list_cpxtab_dl_pow_kernel(
     nc = tc.nc
     with ExitStack() as ctx:
         keep = ctx.enter_context(tc.tile_pool(name="keep", bufs=1))
+        shared = ctx.enter_context(tc.tile_pool(name="shared", bufs=1))
         psum = ctx.enter_context(tc.psum_pool(name="psum", bufs=1))
 
         def sb(shape, dtype, name, **kw):
             return keep.tile(shape, dtype, name=name, align_bytes=64, **kw)
+
+        def placed(shape, dtype, name, offset):
+            return shared.tile(shape, dtype, name=name, align_bytes=64, offset=offset)
 
         def zeroed_plane(name, width):
             plane = sb([P, width], U8, name, tag=name)
@@ -63,7 +68,7 @@ def tile_list_cpxtab_dl_pow_kernel(
         wr4_plane = zeroed_plane("wr4_plane", N)
         nc.vector.memset(tab2_rows[: P - BLOCKS, :].bitcast(I32), 0)
         v2_scales = zeroed_plane("v2_scales", J)
-        tab_codes = sb([P, T], I32, "tab_codes", tag="tab_codes")
+        tab_codes = placed([P, T], I32, "tab_codes", TAB_AT)
         load_words(tab_codes, tab_words, slice(0, HEAD))
         fill_plane([nc.sync] * ROWS, tab_plane, tab_scales[0])
         load_words(tab_codes, tab_words, slice(HEAD, T))
@@ -72,7 +77,7 @@ def tile_list_cpxtab_dl_pow_kernel(
         wr4_codes = sb([P, 2 * N], U8, "wr4_codes")
         nc.sync.dma_start(out=wr4_codes[:].bitcast(I32), in_=wr4_words[0].bitcast(I32))
         fill_plane([nc.sync] * ROWS, wr4_plane, wr4_scales[0])
-        wrd_raw = sb([P, PACK, N], F32, "wrd_raw", tag="wrd_raw")
+        wrd_raw = placed([P, PACK, N], F32, "wrd_raw", WRD_AT)
         load_weight(wrd_raw, wrd)
         tab2_codes = sb([P, T], I32, "tab2_codes")
         load_words(tab2_codes, tab2_words, slice(0, T))
@@ -120,14 +125,14 @@ def tile_list_cpxtab_dl_pow_kernel(
         gather(third_scales[:], tab_plane[:], 2 * SLICE, SLICE)
         v.append((v_codes[:, 2 * SLICE :], third_scales[:]))
         wrd_q = quantised(rounded(wrd_raw, "wrd"), "wrd")
-        minus_wi_bf16 = sb([P, N, PACK], BF16, "minus_wi_bf16", tag="wrd_raw")
+        minus_wi_bf16 = placed([P, N, PACK], BF16, "minus_wi_bf16", WRD_AT)
         nc.scalar.activation(
             minus_wi_bf16[:].rearrange("p n i -> p (n i)"), wi_bf16[:].rearrange("p n i -> p (n i)"), ACT.Copy, scale=-1.0
         )
-        first_codes = sb([P, SLICE], U32, "v2_codes0", tag="wrd_bf16")
+        first_codes = placed([P, SLICE], U32, "v2_codes0", WRD_AT + 2 * N * PACK)
         gather(first_codes[:], tab2_codes[:].bitcast(U32), 0, SLICE)
         minus_wi_q = quantised(minus_wi_bf16, "minus_wi")
-        later_codes = sb([P, LAST * SLICE], U32, "v2_codes", tag="wrd_raw")
+        later_codes = sb([P, LAST * SLICE], U32, "v2_codes", tag="wi_bf16")
 
         def e4m3_pass(dst, weight, m, moving, cols, stop=False):
             (w_codes, w_plane), (codes, scales) = weight, moving
@@ -201,12 +206,15 @@ def tile_list_cpxtab_dl_pow_kernel(
                 nc.scalar.activation(slice_squares[:, i].rearrange("p z j -> p (z j)"), both, ACT.Square)
 
         out_rows = out.rearrange("(m p) j -> p m j", p=P)
-        held_behind = {(1, 1): "tab_plane", (2, 0): "tab_codes"}
         for s in range(LAST):
             for m in range(ROW_TILES):
                 adder = nc.gpsimd if s * ROW_TILES + m < GPSIMD_PIECES else nc.vector
                 name = "power%d_%d" % (s, m)
-                power = sb([P, SLICE], F32, name, tag=held_behind.get((s, m), name))
+                piece = s * ROW_TILES + m - GPSIMD_PIECES
+                if 0 <= piece < 2:
+                    power = placed([P, SLICE], F32, name, TAB_AT + 4 * SLICE * piece)
+                else:
+                    power = sb([P, SLICE], F32, name)
                 adder.tensor_tensor(power[:], squares[s][:, m, 0, :], squares[s][:, m, 1, :], ALU.add)
                 nc.sync.dma_start(out=out_rows[:, m, s * SLICE : (s + 1) * SLICE], in_=power[:])
         half = SLICE // 2

@@ -26,7 +26,7 @@ BANK, BANKS = 512, 8
 GPSIMD_PIECES = 3
 E2M1_N = 128
 HEAD = T // 4
-WRD_AT, TAB_AT = 0, 4 * N * PACK
+WRD_AT, WI_AT, TAB_AT = 0, 4 * N * PACK, 8 * N * PACK
 RUN = 4
 
 
@@ -50,9 +50,9 @@ def tile_list_cpxtab_dl_pow_kernel(
             nc.vector.memset(plane[:].bitcast(I32), 0)
             return plane
 
-        def fill_plane(queues, plane, rows):
+        def fill_plane(plane, rows):
             for r in range(ROWS):
-                queues[r].dma_start(out=plane[r:P:QUADRANT, :].bitcast(I32), in_=rows[r:BLOCKS:ROWS, :].bitcast(I32))
+                nc.sync.dma_start(out=plane[r:P:QUADRANT, :].bitcast(I32), in_=rows[r:BLOCKS:ROWS, :].bitcast(I32))
 
         def load_words(tile, words, cols):
             nc.sync.dma_start(out=tile[:, cols], in_=words[0].rearrange("p t i -> p (t i)").bitcast(I32)[:, cols])
@@ -70,13 +70,13 @@ def tile_list_cpxtab_dl_pow_kernel(
         v2_scales = zeroed_plane("v2_scales", J)
         tab_codes = placed([P, T], I32, "tab_codes", TAB_AT)
         load_words(tab_codes, tab_words, slice(0, HEAD))
-        fill_plane([nc.sync] * ROWS, tab_plane, tab_scales[0])
+        fill_plane(tab_plane[:], tab_scales[0])
         load_words(tab_codes, tab_words, slice(HEAD, T))
-        wi_raw = sb([P, PACK, N], F32, "wi_raw", tag="wi_raw")
-        load_weight(wi_raw, wi)
         wr4_codes = sb([P, 2 * N], U8, "wr4_codes")
         nc.sync.dma_start(out=wr4_codes[:].bitcast(I32), in_=wr4_words[0].bitcast(I32))
-        fill_plane([nc.sync] * ROWS, wr4_plane, wr4_scales[0])
+        fill_plane(wr4_plane[:], wr4_scales[0])
+        wi_raw = placed([P, PACK, N], F32, "wi_raw", WI_AT)
+        load_weight(wi_raw, wi)
         wrd_raw = placed([P, PACK, N], F32, "wrd_raw", WRD_AT)
         load_weight(wrd_raw, wrd)
         tab2_codes = sb([P, T], I32, "tab2_codes")
@@ -102,9 +102,12 @@ def tile_list_cpxtab_dl_pow_kernel(
             )
             return codes, plane
 
-        v2_rows = sb([P, J], U8, "v2_rows")
-        gather(v2_rows[:], tab2_rows[:], 0, J)
-        fill_plane([nc.sync] * ROWS, v2_scales, v2_rows[P - BLOCKS :, :])
+        def v2_scale_bytes(rows, j0):
+            count = rows.shape[1]
+            gather(rows[:], tab2_rows[:], j0, count)
+            fill_plane(v2_scales[:, j0 : j0 + count], rows[P - BLOCKS :, :])
+
+        v2_scale_bytes(sb([P, LAST * SLICE], U8, "v2_rows"), 0)
 
         def gather_v(s, codes, scales):
             gather(codes, tab_codes[:].bitcast(U32), s * SLICE, SLICE)
@@ -121,8 +124,9 @@ def tile_list_cpxtab_dl_pow_kernel(
             v.append((v_codes[:, j0 : j0 + SLICE], early_scales[:, j0 : j0 + SLICE]))
         wi_bf16 = rounded(wi_raw, "wi")
         wi_q = quantised(wi_bf16, "wi")
-        third_scales = sb([P, SLICE], U8, "v_scales2", tag="wi_raw")
+        third_scales = placed([P, SLICE], U8, "v_scales2", WI_AT)
         gather(third_scales[:], tab_plane[:], 2 * SLICE, SLICE)
+        v2_scale_bytes(placed([P, SLICE], U8, "v2_rows_last", WI_AT + SLICE), LAST * SLICE)
         v.append((v_codes[:, 2 * SLICE :], third_scales[:]))
         wrd_q = quantised(rounded(wrd_raw, "wrd"), "wrd")
         minus_wi_bf16 = placed([P, N, PACK], BF16, "minus_wi_bf16", WRD_AT)

@@ -25,8 +25,11 @@ LAST = SLICES - 1
 BANK, BANKS = 512, 8
 GPSIMD_PIECES = 3
 E2M1_N = 128
-HEAD = T // 4
-WRD_AT, WI_AT, TAB_AT = 0, 4 * N * PACK, 8 * N * PACK
+EARLY = 640
+WRD_AT = 0
+TAB_AT = WRD_AT + 4 * N * PACK
+LATER_AT = TAB_AT + 4 * T
+ROWS_AT = LATER_AT + 4 * LAST * SLICE - 64
 RUN = 4
 
 
@@ -54,8 +57,8 @@ def tile_list_cpxtab_dl_pow_kernel(
             for r in range(ROWS):
                 nc.sync.dma_start(out=plane[r:P:QUADRANT, :].bitcast(I32), in_=rows[r:BLOCKS:ROWS, :].bitcast(I32))
 
-        def load_words(tile, words, cols):
-            nc.sync.dma_start(out=tile[:, cols], in_=words[0].rearrange("p t i -> p (t i)").bitcast(I32)[:, cols])
+        def load_words(tile, words):
+            nc.sync.dma_start(out=tile[:], in_=words[0].rearrange("p t i -> p (t i)").bitcast(I32))
 
         def load_weight(raw, w):
             nc.sync.dma_start(out=raw[:], in_=w.rearrange("(p i) n -> p i n", i=PACK))
@@ -68,35 +71,31 @@ def tile_list_cpxtab_dl_pow_kernel(
         wr4_plane = zeroed_plane("wr4_plane", N)
         nc.vector.memset(tab2_rows[: P - BLOCKS, :].bitcast(I32), 0)
         v2_scales = zeroed_plane("v2_scales", J)
-        tab_codes = placed([P, T], I32, "tab_codes", TAB_AT)
-        load_words(tab_codes, tab_words, slice(0, HEAD))
+        wi_raw = sb([P, PACK, N], F32, "wi_raw", tag="wi_raw")
+        load_weight(wi_raw, wi)
         fill_plane(tab_plane[:], tab_scales[0])
-        load_words(tab_codes, tab_words, slice(HEAD, T))
+        tab_codes = placed([P, T], I32, "tab_codes", TAB_AT)
+        load_words(tab_codes, tab_words)
+        wrd_raw = placed([P, PACK, N], F32, "wrd_raw", WRD_AT)
+        load_weight(wrd_raw, wrd)
         wr4_codes = sb([P, 2 * N], U8, "wr4_codes")
         nc.sync.dma_start(out=wr4_codes[:].bitcast(I32), in_=wr4_words[0].bitcast(I32))
         fill_plane(wr4_plane[:], wr4_scales[0])
-        wi_raw = placed([P, PACK, N], F32, "wi_raw", WI_AT)
-        load_weight(wi_raw, wi)
-        wrd_raw = placed([P, PACK, N], F32, "wrd_raw", WRD_AT)
-        load_weight(wrd_raw, wrd)
         tab2_codes = sb([P, T], I32, "tab2_codes")
-        load_words(tab2_codes, tab2_words, slice(0, T))
+        load_words(tab2_codes, tab2_words)
 
         def gather(dst, window, j0, count):
             nc.vector.tensor_copy(dst, window.indirect(offsets[:, j0 // STRIPE : (j0 + count) // STRIPE]))
 
-        def rounded(raw, name):
-            grouped = sb([P, N, PACK], BF16, name + "_bf16", tag=name + "_bf16")
+        def round_weight(grouped, raw):
             nc.scalar.activation(
-                grouped[:].rearrange("p (c e) i -> p c i e", e=RUN),
+                grouped.rearrange("p (c e) i -> p c i e", e=RUN),
                 raw[:].rearrange("p i (c e) -> p c i e", e=RUN),
                 ACT.Copy,
             )
-            return grouped
 
-        def quantised(grouped, name):
+        def quantised(grouped, name, plane):
             codes = sb([P, N], U32, name + "_codes")
-            plane = sb([P, N], U8, name + "_plane")
             nc.vector.quantize_mx(
                 out=codes[:].bitcast(E4M3), scales=plane[:], in_=grouped[:].rearrange("p n i -> p (n i)")
             )
@@ -107,38 +106,30 @@ def tile_list_cpxtab_dl_pow_kernel(
             gather(rows[:], tab2_rows[:], j0, count)
             fill_plane(v2_scales[:, j0 : j0 + count], rows[P - BLOCKS :, :])
 
-        v2_scale_bytes(sb([P, LAST * SLICE], U8, "v2_rows"), 0)
-
-        def gather_v(s, codes, scales):
-            gather(codes, tab_codes[:].bitcast(U32), s * SLICE, SLICE)
-            gather(scales, tab_plane[:], s * SLICE, SLICE)
-            return codes, scales
-
-        v = []
-        early_scales = sb([P, 2 * SLICE], U8, "v_scales")
-        gather(early_scales[:], tab_plane[:], 0, 2 * SLICE)
-        v_codes = sb([P, LAST * SLICE], U32, "v_codes")
-        for j0 in range(0, LAST * SLICE, SLICE):
-            gather(v_codes[:, j0 : j0 + SLICE], tab_codes[:].bitcast(U32), j0, SLICE)
-        for j0 in range(0, 2 * SLICE, SLICE):
-            v.append((v_codes[:, j0 : j0 + SLICE], early_scales[:, j0 : j0 + SLICE]))
-        wi_bf16 = rounded(wi_raw, "wi")
-        wi_q = quantised(wi_bf16, "wi")
-        third_scales = placed([P, SLICE], U8, "v_scales2", WI_AT)
-        gather(third_scales[:], tab_plane[:], 2 * SLICE, SLICE)
-        v2_scale_bytes(placed([P, SLICE], U8, "v2_rows_last", WI_AT + SLICE), LAST * SLICE)
-        v.append((v_codes[:, 2 * SLICE :], third_scales[:]))
-        wrd_q = quantised(rounded(wrd_raw, "wrd"), "wrd")
-        minus_wi_bf16 = placed([P, N, PACK], BF16, "minus_wi_bf16", WRD_AT)
+        v2_scale_bytes(placed([P, EARLY], U8, "v2_rows", ROWS_AT), 0)
+        early_scales = sb([P, LAST * SLICE], U8, "v_scales")
+        gather(early_scales[:], tab_plane[:], 0, LAST * SLICE)
+        wi_bf16 = sb([P, N, PACK], BF16, "wi_bf16")
+        round_weight(wi_bf16[:], wi_raw)
+        wi_q = quantised(wi_bf16, "wi", sb([P, N], U8, "wi_plane"))
+        minus_wi_bf16 = sb([P, N, PACK], BF16, "minus_wi_bf16")
         nc.scalar.activation(
             minus_wi_bf16[:].rearrange("p n i -> p (n i)"), wi_bf16[:].rearrange("p n i -> p (n i)"), ACT.Copy, scale=-1.0
         )
-        first_codes = placed([P, SLICE], U32, "v2_codes0", WRD_AT + 2 * N * PACK)
+        v_codes = sb([P, LAST * SLICE], U32, "v_codes", tag="wi_raw")
+        for j0 in range(0, LAST * SLICE, SLICE):
+            gather(v_codes[:, j0 : j0 + SLICE], tab_codes[:].bitcast(U32), j0, SLICE)
+        v = [(v_codes[:, j0 : j0 + SLICE], early_scales[:, j0 : j0 + SLICE]) for j0 in range(0, LAST * SLICE, SLICE)]
+        wrd_bf16 = sb([P, N, PACK], BF16, "wrd_bf16")
+        round_weight(wrd_bf16[:], wrd_raw)
+        wrd_q = quantised(wrd_bf16, "wrd", sb([P, N], U8, "wrd_plane"))
+        v2_scale_bytes(placed([P, J - EARLY], U8, "v2_rows_last", WRD_AT), EARLY)
+        first_codes = sb([P, SLICE], U32, "v2_codes0")
         gather(first_codes[:], tab2_codes[:].bitcast(U32), 0, SLICE)
-        minus_wi_q = quantised(minus_wi_bf16, "minus_wi")
-        later_codes = sb([P, LAST * SLICE], U32, "v2_codes", tag="wi_bf16")
+        minus_wi_q = quantised(minus_wi_bf16, "minus_wi", placed([P, N], U8, "minus_wi_plane", ROWS_AT + 64))
+        later_codes = placed([P, LAST * SLICE], U32, "v2_codes", LATER_AT)
 
-        def e4m3_pass(dst, weight, m, moving, cols, stop=False):
+        def e4m3_pass(dst, weight, m, moving, cols, start=False, stop=False):
             (w_codes, w_plane), (codes, scales) = weight, moving
             nc.tensor.matmul_mx(
                 out=dst,
@@ -146,7 +137,7 @@ def tile_list_cpxtab_dl_pow_kernel(
                 lhsT_scale=w_plane[:, m * M : (m + 1) * M],
                 rhs=codes[:, cols].bitcast(E4M3),
                 rhs_scale=scales[:, cols],
-                start=False,
+                start=start,
                 stop=stop,
             )
 
@@ -164,33 +155,40 @@ def tile_list_cpxtab_dl_pow_kernel(
                     stop=False,
                 )
 
-        squares = []
-        banks_used = 0
-        for s in range(SLICES):
-            j0 = s * SLICE
+        def bank_pieces(s):
             width = SLICE if s < LAST else SLICE // 2
             pieces = []
             for m in range(ROW_TILES):
                 for c0 in range(0, SLICE, width):
-                    bank = psum.tile([P, BANK], F32, name="bank%d" % banks_used, tag="bank%d" % (banks_used % BANKS))
+                    number = s * ROW_TILES + len(pieces)
+                    bank = psum.tile([P, BANK], F32, name="bank%d" % number, tag="bank%d" % (number % BANKS))
                     pieces.append((m, slice(c0, c0 + width), bank[:, :width], bank[:, width : 2 * width], bank[:, : 2 * width]))
-                    banks_used = banks_used + 1
+            return pieces
+
+        early = [bank_pieces(s) for s in range(LAST)]
+        for s in range(2):
+            for m, cols, zr, zi, both in early[s]:
+                e4m3_pass(zi, wi_q, m, v[s], cols, start=True)
+        for s in range(LAST):
+            for m, cols, zr, zi, both in early[s]:
+                wr4_passes(zr, m, v[s], cols, start=s == 2)
+        for m, cols, zr, zi, both in early[2]:
+            e4m3_pass(zi, wi_q, m, v[2], cols)
+        for s in range(LAST):
+            for m, cols, zr, zi, both in early[s]:
+                e4m3_pass(zr, wrd_q, m, v[s], cols)
+
+        squares = []
+        for s in range(SLICES):
+            j0 = s * SLICE
+            pieces = early[s] if s < LAST else bank_pieces(s)
+            width = SLICE * ROW_TILES // len(pieces)
             v2 = (later_codes[:, j0 - SLICE : j0] if s else first_codes[:], v2_scales[:, j0 : j0 + SLICE])
             if s < LAST:
-                for m, cols, zr, zi, both in pieces:
-                    wr4_passes(zr, m, v[s], cols, start=True)
-                for m, cols, zr, zi, both in pieces:
-                    e4m3_pass(zi, wi_q, m, v[s], cols)
-                behind = (1,) if s == 0 else ()
-                for m, cols, zr, zi, both in pieces:
-                    if m not in behind:
-                        e4m3_pass(zr, wrd_q, m, v[s], cols)
                 if s:
                     gather(v2[0], tab2_codes[:].bitcast(U32), j0, SLICE)
                 for m, cols, zr, zi, both in pieces:
                     wr4_passes(zi, m, v2, cols)
-                    if m in behind:
-                        e4m3_pass(zr, wrd_q, m, v[s], cols)
                     e4m3_pass(zi, wrd_q, m, v2, cols)
                     e4m3_pass(zr, minus_wi_q, m, v2, cols, stop=True)
             else:
@@ -199,7 +197,9 @@ def tile_list_cpxtab_dl_pow_kernel(
                     wr4_passes(zi, m, v2, cols, start=True)
                     e4m3_pass(zi, wrd_q, m, v2, cols)
                     e4m3_pass(zr, minus_wi_q, m, v2, cols)
-                last_v = gather_v(s, v[0][0], v[0][1])
+                last_v = (placed([P, SLICE], U32, "v_codes3", ROWS_AT + 64 + 2 * SLICE)[:], placed([P, SLICE], U8, "v_scales3", ROWS_AT + 64 + SLICE)[:])
+                gather(last_v[0], tab_codes[:].bitcast(U32), j0, SLICE)
+                gather(last_v[1], tab_plane[:], j0, SLICE)
                 for m, cols, zr, zi, both in pieces:
                     wr4_passes(zr, m, last_v, cols)
                     e4m3_pass(zr, wrd_q, m, last_v, cols)

@@ -90,7 +90,7 @@ def tile_list_cpxtab_dl_pow_kernel(
         def round_weight(grouped, raw):
             nc.scalar.activation(
                 grouped.rearrange("p (c e) i -> p c i e", e=RUN),
-                raw[:].rearrange("p i (c e) -> p c i e", e=RUN),
+                raw.rearrange("p i (c e) -> p c i e", e=RUN),
                 ACT.Copy,
             )
 
@@ -110,7 +110,7 @@ def tile_list_cpxtab_dl_pow_kernel(
         early_scales = sb([P, LAST * SLICE], U8, "v_scales")
         gather(early_scales[:], tab_plane[:], 0, LAST * SLICE)
         wi_bf16 = sb([P, N, PACK], BF16, "wi_bf16")
-        round_weight(wi_bf16[:], wi_raw)
+        round_weight(wi_bf16[:], wi_raw[:])
         wi_q = quantised(wi_bf16, "wi", sb([P, N], U8, "wi_plane"))
         minus_wi_bf16 = sb([P, N, PACK], BF16, "minus_wi_bf16")
         nc.scalar.activation(
@@ -121,9 +121,12 @@ def tile_list_cpxtab_dl_pow_kernel(
             gather(v_codes[:, j0 : j0 + SLICE], tab_codes[:].bitcast(U32), j0, SLICE)
         v = [(v_codes[:, j0 : j0 + SLICE], early_scales[:, j0 : j0 + SLICE]) for j0 in range(0, LAST * SLICE, SLICE)]
         wrd_bf16 = sb([P, N, PACK], BF16, "wrd_bf16")
-        round_weight(wrd_bf16[:], wrd_raw)
-        wrd_q = quantised(wrd_bf16, "wrd", sb([P, N], U8, "wrd_plane"))
+        round_weight(wrd_bf16[:, :M, :], wrd_raw[:, :, :M])
+        nc.gpsimd.tensor_scalar(
+            wrd_bf16[:, M:, :], wrd_raw[:, :, M:].rearrange("p i n -> p n i"), 1.0, 0.0, ALU.mult, ALU.add
+        )
         v2_scale_bytes(placed([P, J - EARLY], U8, "v2_rows_last", WRD_AT), EARLY)
+        wrd_q = quantised(wrd_bf16, "wrd", sb([P, N], U8, "wrd_plane"))
         first_codes = sb([P, SLICE], U32, "v2_codes0")
         gather(first_codes[:], tab2_codes[:].bitcast(U32), 0, SLICE)
         minus_wi_q = quantised(minus_wi_bf16, "minus_wi", placed([P, N], U8, "minus_wi_plane", ROWS_AT + 64))

@@ -159,9 +159,9 @@ def tile_list_cpxtab_dl_pow_kernel(
                 )
 
         def bank_pieces(s):
-            width = SLICE if s < LAST else SLICE // 2
             pieces = []
             for m in range(ROW_TILES):
+                width = SLICE // 2 if (s, m) == (LAST, ROW_TILES - 1) else SLICE
                 for c0 in range(0, SLICE, width):
                     number = s * ROW_TILES + len(pieces)
                     bank = psum.tile([P, BANK], F32, name="bank%d" % number, tag="bank%d" % (number % BANKS))
@@ -177,62 +177,62 @@ def tile_list_cpxtab_dl_pow_kernel(
                 wr4_passes(zr, m, v[s], cols, start=s == 2)
         for m, cols, zr, zi, both in early[2]:
             e4m3_pass(zi, wi_q, m, v[2], cols)
-        for s in range(LAST):
-            for m, cols, zr, zi, both in early[s]:
-                e4m3_pass(zr, wrd_q, m, v[s], cols)
+        for m, cols, zr, zi, both in early[0]:
+            e4m3_pass(zr, wrd_q, m, v[0], cols)
 
-        squares = []
+        def v2_base(piece, v2, start=False):
+            m, cols, zr, zi, both = piece
+            wr4_passes(zi, m, v2, cols, start=start)
+
+        def v2_passes(piece, v2, stop=False):
+            m, cols, zr, zi, both = piece
+            e4m3_pass(zi, wrd_q, m, v2, cols)
+            e4m3_pass(zr, minus_wi_q, m, v2, cols, stop=stop)
+
+        def v_passes(piece, last_v, stop=False):
+            m, cols, zr, zi, both = piece
+            wr4_passes(zr, m, last_v, cols)
+            e4m3_pass(zr, wrd_q, m, last_v, cols)
+            e4m3_pass(zi, wi_q, m, last_v, cols, stop=stop)
+
+        squared = []
         for s in range(SLICES):
             j0 = s * SLICE
-            pieces = early[s] if s < LAST else bank_pieces(s)
-            width = SLICE * ROW_TILES // len(pieces)
             v2 = (later_codes[:, j0 - SLICE : j0] if s else first_codes[:], v2_scales[:, j0 : j0 + SLICE])
-            if s < LAST:
-                if s:
-                    gather(v2[0], tab2_codes[:].bitcast(U32), j0, SLICE)
-                for m, cols, zr, zi, both in pieces:
-                    wr4_passes(zi, m, v2, cols)
-                    e4m3_pass(zi, wrd_q, m, v2, cols)
-                    e4m3_pass(zr, minus_wi_q, m, v2, cols, stop=True)
-            else:
+            if s:
                 gather(v2[0], tab2_codes[:].bitcast(U32), j0, SLICE)
-                for m, cols, zr, zi, both in pieces:
-                    wr4_passes(zi, m, v2, cols, start=True)
-                    e4m3_pass(zi, wrd_q, m, v2, cols)
-                    e4m3_pass(zr, minus_wi_q, m, v2, cols)
-                last_v = (placed([P, SLICE], U32, "v_codes3", ROWS_AT + 64 + 2 * SLICE)[:], placed([P, SLICE], U8, "v_scales3", ROWS_AT + 64 + SLICE)[:])
-                gather(last_v[0], tab_codes[:].bitcast(U32), j0, SLICE)
-                gather(last_v[1], tab_plane[:], j0, SLICE)
-                for m, cols, zr, zi, both in pieces:
-                    wr4_passes(zr, m, last_v, cols)
-                    e4m3_pass(zr, wrd_q, m, last_v, cols)
-                    e4m3_pass(zi, wi_q, m, last_v, cols, stop=True)
-            slice_squares = sb([P, len(pieces), 2, width], F32, "squares%d" % s)
-            squares.append(slice_squares)
-            for i, (m, cols, zr, zi, both) in enumerate(pieces):
-                nc.scalar.activation(slice_squares[:, i].rearrange("p z j -> p (z j)"), both, ACT.Square)
+            if s < LAST:
+                pieces = early[s]
+                for piece in pieces:
+                    v2_base(piece, v2)
+                    if s:
+                        e4m3_pass(piece[2], wrd_q, piece[0], v[s], piece[1])
+                    v2_passes(piece, v2, stop=True)
+            else:
+                pieces = bank_pieces(s)
+                for piece in pieces:
+                    v2_base(piece, v2, start=True)
+                v2_passes(pieces[0], v2)
+                last_codes = placed([P, SLICE], U32, "v_codes3", ROWS_AT + 64 + 2 * SLICE)
+                last_scales = placed([P, SLICE], U8, "v_scales3", ROWS_AT + 64 + SLICE)
+                gather(last_codes[:], tab_codes[:].bitcast(U32), j0, SLICE)
+                gather(last_scales[:], tab_plane[:], j0, SLICE)
+                last_v = (last_codes[:], last_scales[:])
+                v_passes(pieces[0], last_v, stop=True)
+                for piece in pieces[1:]:
+                    v_passes(piece, last_v)
+                    v2_passes(piece, v2, stop=True)
+            for m, cols, zr, zi, both in pieces:
+                squares = sb([P, 2, zr.shape[1]], F32, "squares%d" % len(squared))
+                nc.scalar.activation(squares[:].rearrange("p z j -> p (z j)"), both, ACT.Square)
+                squared.append((m, slice(j0 + cols.start, j0 + cols.stop), squares))
 
         out_rows = out.rearrange("(m p) j -> p m j", p=P)
-        for s in range(LAST):
-            for m in range(ROW_TILES):
-                adder = nc.gpsimd if s * ROW_TILES + m < GPSIMD_PIECES else nc.vector
-                name = "power%d_%d" % (s, m)
-                piece = s * ROW_TILES + m - GPSIMD_PIECES
-                if 0 <= piece < 2:
-                    power = placed([P, SLICE], F32, name, TAB_AT + 4 * SLICE * piece)
-                else:
-                    power = sb([P, SLICE], F32, name)
-                adder.tensor_tensor(power[:], squares[s][:, m, 0, :], squares[s][:, m, 1, :], ALU.add)
-                nc.sync.dma_start(out=out_rows[:, m, s * SLICE : (s + 1) * SLICE], in_=power[:])
-        half = SLICE // 2
-        power = sb([P, ROW_TILES, SLICE], F32, "power_last")
-        for m in range(ROW_TILES):
-            for h in range(2):
-                cols = slice(h * half, (h + 1) * half)
-                piece = squares[LAST][:, 2 * m + h]
-                nc.vector.tensor_tensor(power[:, m, cols], piece[:, 0, :], piece[:, 1, :], ALU.add)
-                if m == ROW_TILES - 1:
-                    j0 = J - SLICE + h * half
-                    nc.sync.dma_start(out=out_rows[:, m, j0 : j0 + half], in_=power[:, m, cols])
-            if m < ROW_TILES - 1:
-                nc.sync.dma_start(out=out_rows[:, m, J - SLICE :], in_=power[:, m, :])
+        for number, (m, cols, squares) in enumerate(squared):
+            name = "power%d" % number
+            shape = [P, squares.shape[2]]
+            held = number - GPSIMD_PIECES
+            power = placed(shape, F32, name, TAB_AT + 4 * SLICE * held) if 0 <= held < 2 else sb(shape, F32, name)
+            adder = nc.gpsimd if held < 0 else nc.vector
+            adder.tensor_tensor(power[:], squares[:, 0, :], squares[:, 1, :], ALU.add)
+            nc.sync.dma_start(out=out_rows[:, m, cols], in_=power[:])

@@ -24,7 +24,7 @@ SLICES = J // SLICE
 LAST = SLICES - 1
 BANK, BANKS = 512, 8
 GPSIMD_PIECES = 3
-E2M1_N = 128
+E2M1_N = 256
 EARLY = 640
 WRD_AT = 0
 TAB_AT = WRD_AT + 4 * N * PACK
@@ -146,10 +146,11 @@ def tile_list_cpxtab_dl_pow_kernel(
 
         def wr4_passes(dst, m, moving, cols, start=False):
             codes, scales = moving
-            for c0 in range(0, dst.shape[1], E2M1_N):
-                part = slice(cols.start + c0, cols.start + c0 + E2M1_N)
+            width = min(E2M1_N, dst.shape[1])
+            for c0 in range(0, dst.shape[1], width):
+                part = slice(cols.start + c0, cols.start + c0 + width)
                 nc.tensor.matmul_mx(
-                    out=dst[:, c0 : c0 + E2M1_N],
+                    out=dst[:, c0 : c0 + width],
                     lhsT=wr4_codes[:, 2 * m * M : 2 * (m + 1) * M].bitcast(E2M1),
                     lhsT_scale=wr4_plane[:, m * M : (m + 1) * M],
                     rhs=codes[:, part].bitcast(E4M3),

@@ -66,7 +66,7 @@ def tile_list_cpxtab_dl_pow_kernel(
         offsets = keep.tile([P, J // STRIPE], U16, name="offsets")
         nc.sync.dma_start(offsets[:], offs)
         tab2_rows = sb([P, T], U8, "tab2_rows")
-        nc.sync.dma_start(out=tab2_rows[P - BLOCKS :, :].bitcast(I32), in_=tab2_scales[0].bitcast(I32))
+        nc.scalar.dma_start(out=tab2_rows[P - BLOCKS :, :].bitcast(I32), in_=tab2_scales[0].bitcast(I32))
         tab_plane = zeroed_plane("tab_plane", T)
         wr4_plane = zeroed_plane("wr4_plane", N)
         nc.vector.memset(tab2_rows[: P - BLOCKS, :].bitcast(I32), 0)

from contextlib import ExitStack

import concourse.mybir as mybir

K, N, T, J = 512, 256, 2048, 1024
FLOPS = 6 * 2 * K * N * J

F32, BF16 = mybir.dt.float32, mybir.dt.bfloat16
I32, U32, U16, U8 = mybir.dt.int32, mybir.dt.uint32, mybir.dt.uint16, mybir.dt.uint8
E4M3, E2M1 = mybir.dt.float8_e4m3fn_x4, mybir.dt.float4_e2m1fn_x4
ACT = mybir.ActivationFunctionType
ALU = mybir.AluOpType

P = 128
PACK = 4
QUADRANT = 32
ROWS = 4
BLOCKS = K // 32
STRIPE = 16
M = 128
ROW_TILES = N // M
SLICE = 256
SLICES = J // SLICE
LAST = SLICES - 1
BANK, BANKS = 512, 8
GPSIMD_PIECES = 3
E2M1_N = 256
EARLY = 640
WRD_AT = 0
TAB_AT = WRD_AT + 4 * N * PACK
LATER_AT = TAB_AT + 4 * T
ROWS_AT = LATER_AT + 4 * LAST * SLICE - 64
RUN = 4


def tile_list_cpxtab_dl_pow_kernel(
    tc, tab_words, tab_scales, tab2_words, tab2_scales, wr4_words, wr4_scales, wrd, wi, offs, out
):
    nc = tc.nc
    with ExitStack() as ctx:
        keep = ctx.enter_context(tc.tile_pool(name="keep", bufs=1))
        shared = ctx.enter_context(tc.tile_pool(name="shared", bufs=1))
        psum = ctx.enter_context(tc.psum_pool(name="psum", bufs=1))

        def sb(shape, dtype, name, **kw):
            return keep.tile(shape, dtype, name=name, align_bytes=64, **kw)

        def placed(shape, dtype, name, offset):
            return shared.tile(shape, dtype, name=name, align_bytes=64, offset=offset)

        def zeroed_plane(name, width):
            plane = sb([P, width], U8, name, tag=name)
            nc.vector.memset(plane[:].bitcast(I32), 0)
            return plane

        def fill_plane(plane, rows):
            for r in range(ROWS):
                nc.sync.dma_start(out=plane[r:P:QUADRANT, :].bitcast(I32), in_=rows[r:BLOCKS:ROWS, :].bitcast(I32))

        def load_words(tile, words):
            nc.sync.dma_start(out=tile[:], in_=words[0].rearrange("p t i -> p (t i)").bitcast(I32))

        def load_weight(raw, w):
            nc.sync.dma_start(out=raw[:], in_=w.rearrange("(p i) n -> p i n", i=PACK))

        offsets = keep.tile([P, J // STRIPE], U16, name="offsets")
        nc.sync.dma_start(offsets[:], offs)
        tab2_rows = sb([P, T], U8, "tab2_rows")
        nc.scalar.dma_start(out=tab2_rows[P - BLOCKS :, :].bitcast(I32), in_=tab2_scales[0].bitcast(I32))
        tab_plane = zeroed_plane("tab_plane", T)
        wr4_plane = zeroed_plane("wr4_plane", N)
        nc.vector.memset(tab2_rows[: P - BLOCKS, :].bitcast(I32), 0)
        v2_scales = zeroed_plane("v2_scales", J)
        wi_raw = sb([P, PACK, N], F32, "wi_raw", tag="wi_raw")
        load_weight(wi_raw, wi)
        fill_plane(tab_plane[:], tab_scales[0])
        tab_codes = placed([P, T], I32, "tab_codes", TAB_AT)
        load_words(tab_codes, tab_words)
        wrd_raw = placed([P, PACK, N], F32, "wrd_raw", WRD_AT)
        load_weight(wrd_raw, wrd)
        wr4_codes = sb([P, 2 * N], U8, "wr4_codes")
        nc.sync.dma_start(out=wr4_codes[:].bitcast(I32), in_=wr4_words[0].bitcast(I32))
        fill_plane(wr4_plane[:], wr4_scales[0])
        tab2_codes = sb([P, T], I32, "tab2_codes")
        load_words(tab2_codes, tab2_words)

        def gather(dst, window, j0, count):
            nc.vector.tensor_copy(dst, window.indirect(offsets[:, j0 // STRIPE : (j0 + count) // STRIPE]))

        def round_weight(grouped, raw):
            nc.scalar.activation(
                grouped.rearrange("p (c e) i -> p c i e", e=RUN),
                raw.rearrange("p i (c e) -> p c i e", e=RUN),
                ACT.Copy,
            )

        def quantised(grouped, name, plane):
            codes = sb([P, N], U32, name + "_codes")
            nc.vector.quantize_mx(
                out=codes[:].bitcast(E4M3), scales=plane[:], in_=grouped[:].rearrange("p n i -> p (n i)")
            )
            return codes, plane

        def v2_scale_bytes(rows, j0):
            count = rows.shape[1]
            gather(rows[:], tab2_rows[:], j0, count)
            fill_plane(v2_scales[:, j0 : j0 + count], rows[P - BLOCKS :, :])

        v2_scale_bytes(placed([P, EARLY], U8, "v2_rows", ROWS_AT), 0)
        early_scales = sb([P, LAST * SLICE], U8, "v_scales")
        gather(early_scales[:], tab_plane[:], 0, LAST * SLICE)
        wi_bf16 = sb([P, N, PACK], BF16, "wi_bf16")
        round_weight(wi_bf16[:], wi_raw[:])
        wi_q = quantised(wi_bf16, "wi", sb([P, N], U8, "wi_plane"))
        minus_wi_bf16 = sb([P, N, PACK], BF16, "minus_wi_bf16")
        nc.scalar.activation(
            minus_wi_bf16[:].rearrange("p n i -> p (n i)"), wi_bf16[:].rearrange("p n i -> p (n i)"), ACT.Copy, scale=-1.0
        )
        v_codes = sb([P, LAST * SLICE], U32, "v_codes", tag="wi_raw")
        for j0 in range(0, LAST * SLICE, SLICE):
            gather(v_codes[:, j0 : j0 + SLICE], tab_codes[:].bitcast(U32), j0, SLICE)
        v = [(v_codes[:, j0 : j0 + SLICE], early_scales[:, j0 : j0 + SLICE]) for j0 in range(0, LAST * SLICE, SLICE)]
        wrd_bf16 = sb([P, N, PACK], BF16, "wrd_bf16")
        round_weight(wrd_bf16[:, :M, :], wrd_raw[:, :, :M])
        nc.gpsimd.tensor_scalar(
            wrd_bf16[:, M:, :], wrd_raw[:, :, M:].rearrange("p i n -> p n i"), 1.0, 0.0, ALU.mult, ALU.add
        )
        v2_scale_bytes(placed([P, J - EARLY], U8, "v2_rows_last", WRD_AT), EARLY)
        wrd_q = quantised(wrd_bf16, "wrd", sb([P, N], U8, "wrd_plane"))
        first_codes = sb([P, SLICE], U32, "v2_codes0")
        gather(first_codes[:], tab2_codes[:].bitcast(U32), 0, SLICE)
        minus_wi_q = quantised(minus_wi_bf16, "minus_wi", placed([P, N], U8, "minus_wi_plane", ROWS_AT + 64))
        later_codes = placed([P, LAST * SLICE], U32, "v2_codes", LATER_AT)

        def e4m3_pass(dst, weight, m, moving, cols, start=False, stop=False):
            (w_codes, w_plane), (codes, scales) = weight, moving
            nc.tensor.matmul_mx(
                out=dst,
                lhsT=w_codes[:, m * M : (m + 1) * M].bitcast(E4M3),
                lhsT_scale=w_plane[:, m * M : (m + 1) * M],
                rhs=codes[:, cols].bitcast(E4M3),
                rhs_scale=scales[:, cols],
                start=start,
                stop=stop,
            )

        def wr4_passes(dst, m, moving, cols, start=False):
            codes, scales = moving
            width = min(E2M1_N, dst.shape[1])
            for c0 in range(0, dst.shape[1], width):
                part = slice(cols.start + c0, cols.start + c0 + width)
                nc.tensor.matmul_mx(
                    out=dst[:, c0 : c0 + width],
                    lhsT=wr4_codes[:, 2 * m * M : 2 * (m + 1) * M].bitcast(E2M1),
                    lhsT_scale=wr4_plane[:, m * M : (m + 1) * M],
                    rhs=codes[:, part].bitcast(E4M3),
                    rhs_scale=scales[:, part],
                    start=start and c0 == 0,
                    stop=False,
                )

        def bank_pieces(s):
            pieces = []
            for m in range(ROW_TILES):
                width = SLICE // 2 if (s, m) == (LAST, ROW_TILES - 1) else SLICE
                for c0 in range(0, SLICE, width):
                    number = s * ROW_TILES + len(pieces)
                    bank = psum.tile([P, BANK], F32, name="bank%d" % number, tag="bank%d" % (number % BANKS))
                    pieces.append((m, slice(c0, c0 + width), bank[:, :width], bank[:, width : 2 * width], bank[:, : 2 * width]))
            return pieces

        early = [bank_pieces(s) for s in range(LAST)]
        for s in range(2):
            for m, cols, zr, zi, both in early[s]:
                e4m3_pass(zi, wi_q, m, v[s], cols, start=True)
        for s in range(LAST):
            for m, cols, zr, zi, both in early[s]:
                wr4_passes(zr, m, v[s], cols, start=s == 2)
        for m, cols, zr, zi, both in early[2]:
            e4m3_pass(zi, wi_q, m, v[2], cols)
        for m, cols, zr, zi, both in early[0]:
            e4m3_pass(zr, wrd_q, m, v[0], cols)

        def v2_base(piece, v2, start=False):
            m, cols, zr, zi, both = piece
            wr4_passes(zi, m, v2, cols, start=start)

        def v2_passes(piece, v2, stop=False):
            m, cols, zr, zi, both = piece
            e4m3_pass(zi, wrd_q, m, v2, cols)
            e4m3_pass(zr, minus_wi_q, m, v2, cols, stop=stop)

        def v_passes(piece, last_v, stop=False):
            m, cols, zr, zi, both = piece
            wr4_passes(zr, m, last_v, cols)
            e4m3_pass(zr, wrd_q, m, last_v, cols)
            e4m3_pass(zi, wi_q, m, last_v, cols, stop=stop)

        squared = []
        for s in range(SLICES):
            j0 = s * SLICE
            v2 = (later_codes[:, j0 - SLICE : j0] if s else first_codes[:], v2_scales[:, j0 : j0 + SLICE])
            if s:
                gather(v2[0], tab2_codes[:].bitcast(U32), j0, SLICE)
            if s < LAST:
                pieces = early[s]
                for piece in pieces:
                    v2_base(piece, v2)
                    if s:
                        e4m3_pass(piece[2], wrd_q, piece[0], v[s], piece[1])
                    v2_passes(piece, v2, stop=True)
            else:
                pieces = bank_pieces(s)
                for piece in pieces:
                    v2_base(piece, v2, start=True)
                v2_passes(pieces[0], v2)
                last_codes = placed([P, SLICE], U32, "v_codes3", ROWS_AT + 64 + 2 * SLICE)
                last_scales = placed([P, SLICE], U8, "v_scales3", ROWS_AT + 64 + SLICE)
                gather(last_codes[:], tab_codes[:].bitcast(U32), j0, SLICE)
                gather(last_scales[:], tab_plane[:], j0, SLICE)
                last_v = (last_codes[:], last_scales[:])
                v_passes(pieces[0], last_v, stop=True)
                for piece in pieces[1:]:
                    v_passes(piece, last_v)
                    v2_passes(piece, v2, stop=True)
            for m, cols, zr, zi, both in pieces:
                squares = sb([P, 2, zr.shape[1]], F32, "squares%d" % len(squared))
                nc.scalar.activation(squares[:].rearrange("p z j -> p (z j)"), both, ACT.Square)
                squared.append((m, slice(j0 + cols.start, j0 + cols.stop), squares))

        out_rows = out.rearrange("(m p) j -> p m j", p=P)
        for number, (m, cols, squares) in enumerate(squared):
            name = "power%d" % number
            shape = [P, squares.shape[2]]
            held = number - GPSIMD_PIECES
            power = placed(shape, F32, name, TAB_AT + 4 * SLICE * held) if 0 <= held < 2 else sb(shape, F32, name)
            adder = nc.gpsimd if held < 0 else nc.vector
            adder.tensor_tensor(power[:], squares[:, 0, :], squares[:, 1, :], ALU.add)
            nc.sync.dma_start(out=out_rows[:, m, cols], in_=power[:])
